import numpy as np
import ml_dtypes


def mxq(x, axis, fmt="e4m3"):
    dtype, down = {"e4m3": (ml_dtypes.float8_e4m3fn, 7), "e5m2": (ml_dtypes.float8_e5m2, 14)}[fmt]
    v = np.moveaxis(np.asarray(x, np.float32).astype(ml_dtypes.bfloat16).astype(np.float64), axis, -1)
    blocks = v.reshape(v.shape[:-1] + (-1, 32))
    amax = np.abs(blocks).max(-1, keepdims=True)
    byte = np.maximum(np.where(amax > 0, np.frexp(amax)[1] - 1 + 127, 0) - down, 1)
    scale = np.exp2(byte - 127.0)
    codes = (blocks / scale).astype(np.float32).astype(dtype).astype(np.float64)
    return np.moveaxis((codes * scale).reshape(v.shape), -1, axis)


WIDE = False


def mx_kscale(k):
    if not WIDE:
        return np.ones(k)
    levels = np.array([10, -10, 5, -5, 0])
    if k % 512:
        return np.exp2(np.random.permutation(np.resize(levels, k // 32))).repeat(32)
    a = np.empty((k // 512, 16))
    for p in range(k // 512):
        a[p, :8] = np.random.permutation(np.resize(levels, 8))
        for g in range(8):
            far = levels[np.abs(levels - a[p, g]) >= 10]
            a[p, g + 8] = far[np.random.randint(len(far))]
    return np.exp2(a.ravel()).repeat(32)


def f64(x):
    return np.asarray(x).astype(np.float64)


def striped(idx):
    return np.tile(idx.reshape(-1, 16).T, (8, 1)).astype(np.uint16)


def unstriped(offs):
    return offs[:16].T.reshape(-1).astype(np.int64)


E2M1 = np.array([0.0, 0.5, 1.0, 1.5, 2.0, 3.0, 4.0, 6.0, -0.0, -0.5, -1.0, -1.5, -2.0, -3.0, -4.0, -6.0])


def pack_weight(w, fmt):
    k, n = w.shape
    w = f64(np.asarray(w, np.float32).astype(ml_dtypes.bfloat16)).reshape(k // 32, 32, n)
    amax = np.abs(w).max(1)
    if fmt == "e4m3":
        byte = np.frexp(amax)[1] - 1 + 127 - 7
    else:
        mant, ex = np.frexp(amax / 6.0)
        byte = np.where(mant > 0.5, ex, ex - 1) + 127
    byte = np.clip(np.where(amax > 0, byte, 1), 1, 254)
    scaled = (w * np.exp2(127.0 - byte)[:, None, :]).reshape(k, n).astype(np.float32)
    by_word = np.ascontiguousarray(scaled.reshape(k // 512, 128, 4, n).transpose(0, 1, 3, 2))
    if fmt == "e4m3":
        words = by_word.astype(ml_dtypes.float8_e4m3fn).view(np.uint8)
    else:
        c = by_word.astype(ml_dtypes.float4_e2m1fn).view(np.uint8) & 0xF
        words = (c[..., 0::2] | (c[..., 1::2] << 4)).reshape(k // 512, 128, 2 * n)
    return np.ascontiguousarray(words), np.ascontiguousarray(byte.astype(np.uint8).reshape(k // 512, 16, n))


def unpack_weight(words, scales, fmt):
    g, _, n = scales.shape
    words = np.ascontiguousarray(words).reshape(g, 128, n, -1)
    if fmt == "e4m3":
        vals = words.view(ml_dtypes.float8_e4m3fn).astype(np.float64)
    else:
        nib = np.empty((g, 128, n, 4), np.uint8)
        nib[..., 0::2] = words & 0xF
        nib[..., 1::2] = words >> 4
        vals = E2M1[nib]
    vals = vals * np.repeat(np.exp2(scales.astype(np.float64) - 127.0), 8, axis=1)[..., None]
    return vals.transpose(0, 1, 3, 2).reshape(g * 512, n)


def gelu(v):
    return 0.5 * v * (1.0 + np.tanh(np.sqrt(2.0 / np.pi) * (v + 0.044715 * v**3)))


K, T, S, H, N, T2 = 1024, 2048, 512, 1024, 512, 1024

def setup_inputs():
    n = np.random.standard_normal
    s = mx_kscale(K)[:, None]
    u = mx_kscale(H)[:, None]
    tab_words, tab_scales = pack_weight(n((K, T)) * s, "e4m3")
    tab2_words, tab2_scales = pack_weight(n((K, T)) * s, "e4m3")
    w2_words, w2_scales = pack_weight(1.3 * n((K, H)) / np.sqrt(K) / s, "e2m1")
    w4_words, w4_scales = pack_weight(n((H, N)) / np.sqrt(H) / u, "e2m1")
    return {
        "tab_words": tab_words, "tab_scales": tab_scales,
        "tab2_words": tab2_words, "tab2_scales": tab2_scales,
        "w1": (1.8 * n((K, H)) / np.sqrt(K) / s).astype(np.float32),
        "w2_words": w2_words, "w2_scales": w2_scales,
        "w3": (1.3 * n((K, H)) / np.sqrt(K) / s).astype(np.float32),
        "gain": (np.random.uniform(0.5, 1.7, H) * u[:, 0]).astype(np.float32),
        "bg": (0.7 * n((H, T2)) * u).astype(np.float32),
        "wg1": np.exp(0.3 * n((128, S))).astype(np.float32),
        "wg2": np.exp(0.3 * n((128, S))).astype(np.float32),
        "w4_words": w4_words, "w4_scales": w4_scales,
        "offs": striped(np.random.permutation(T)[:S]),
        "offs2": striped(np.random.permutation(T)[:S]),
        "offs3": striped(np.random.permutation(T2)[:S]),
        "offs4": striped(np.random.permutation(T2)[:S]),
    }

def reference(tab_words, tab_scales, tab2_words, tab2_scales, w1, w2_words, w2_scales, w3, gain, bg, wg1, wg2, w4_words, w4_scales, offs, offs2, offs3, offs4):
    v = unpack_weight(tab_words, tab_scales, "e4m3")[:, unstriped(offs)]
    v2 = unpack_weight(tab2_words, tab2_scales, "e4m3")[:, unstriped(offs2)]
    w2 = unpack_weight(w2_words, w2_scales, "e2m1")
    w4 = unpack_weight(w4_words, w4_scales, "e2m1")
    h1 = np.tanh(mxq(f64(w1), 0, "e4m3").T @ v)
    h2 = np.maximum(w2.T @ v2, mxq(f64(w3), 0, "e4m3").T @ v2)
    pa = np.zeros((H, T2))
    pa[:, unstriped(offs3)] = np.tile(f64(wg1), (H // 128, 1)) * h1
    pb = np.zeros((H, T2))
    pb[:, unstriped(offs4)] = np.tile(f64(wg2), (H // 128, 1)) * h2
    q = pa + pb
    z = f64(gain)[:, None] * q * np.tanh(q) + f64(bg)
    return w4.T @ mxq(z, 0, "e4m3")

@@ -1,0 +1,325 @@
+from contextlib import ExitStack
+
+import concourse.mybir as mybir
+from concourse.masks import make_identity
+
+K, T, S, H, N, T2 = 1024, 2048, 512, 1024, 512, 1024
+FLOPS = 2 * (3 * K * H * S + H * N * T2)
+
+F32 = mybir.dt.float32
+BF16 = mybir.dt.bfloat16
+I32 = mybir.dt.int32
+U32 = mybir.dt.uint32
+U16 = mybir.dt.uint16
+U8 = mybir.dt.uint8
+FP8X4 = mybir.dt.float8_e4m3fn_x4
+FP4X4 = mybir.dt.float4_e2m1fn_x4
+ACT = mybir.ActivationFunctionType
+ALU = mybir.AluOpType
+
+P = 128
+PACK = 4
+K_PASS = P * PACK
+PASSES = K // K_PASS
+SLICES = H // P
+BLOCKS = H // K_PASS
+HALF = 512
+HALVES = T2 // HALF
+QUARTER = 256
+QUARTERS = T2 // QUARTER
+CHUNK = 2 * P
+CHUNKS = H // CHUNK
+
+
+def tile_list_meteor_catalogue_scores_kernel(
+    tc, tab_words, tab_scales, tab2_words, tab2_scales, w1, w2_words, w2_scales, w3, gain, bg, wg1, wg2,
+    w4_words, w4_scales, offs, offs2, offs3, offs4, out,
+):
+    nc = tc.nc
+    with ExitStack() as ctx:
+        lists = ctx.enter_context(tc.tile_pool(name="lists", bufs=1))
+        keep = ctx.enter_context(tc.tile_pool(name="keep", bufs=1))
+        raw_pool = ctx.enter_context(tc.tile_pool(name="raw", bufs=4))
+        ring = ctx.enter_context(tc.tile_pool(name="ring", bufs=2))
+        out_pool = ctx.enter_context(tc.tile_pool(name="outs", bufs=3))
+        psum = ctx.enter_context(tc.psum_pool(name="psum", bufs=1))
+
+        def kept(shape, dtype, name, tag=None):
+            return keep.tile(shape, dtype, name=name, tag=tag or name, align_bytes=64)
+
+        idx = [lists.tile([P, S // 16], U16, name="idx%d" % i) for i in range(4)]
+        table = [[kept([P, T], I32, "tab%d_%d" % (i, a), "big%d" % (2 * i + a)) for a in range(PASSES)] for i in range(2)]
+        tab_plane = kept([P, T], U8, "tab_plane")
+        tab2_plane = kept([P, PASSES * T], U8, "tab2_plane")
+        v_words = [[kept([P, S], U32, "v%d_%d" % (i, a)) for a in range(PASSES)] for i in range(2)]
+        v_plane = kept([P, S], U8, "v_plane")
+        v2_plane = [kept([P, S], U8, "v2_plane%d" % a) for a in range(PASSES)]
+        w2_sb = kept([P, PASSES, 2 * H], U8, "w2_sb")
+        w2_plane = kept([P, PASSES, H], U8, "w2_plane")
+        w4_sb = kept([P, BLOCKS, 2 * N], U8, "w4_sb")
+        w4_plane = kept([P, BLOCKS, N], U8, "w4_plane")
+        wg_sb = [kept([P, S], F32, "wg%d" % i) for i in range(2)]
+        gain_sb = kept([P, BLOCKS, PACK], F32, "gain_sb")
+        page_a = [kept([P, T2], F32, "page_a%d" % i) for i in range(3)]
+        page_b = [kept([P, T2], F32, "page_b%d" % i) for i in range(2)]
+        h1_sb = [kept([P, S], F32, "h1_%d" % i) for i in range(3)]
+        sum2_sb = [kept([P, S], F32, "sum2_%d" % i) for i in range(2)]
+        stage = [kept([P, 2 * PASSES * P * PACK], BF16, "stage%d" % i) for i in range(2)]
+        stage.append(kept([P, PASSES * P * PACK], BF16, "stage2"))
+        widths = [HALF, QUARTER]
+        z_rows = [[kept([P, PACK, HALF], BF16, "z_rows0_%d" % h) for h in range(HALVES)]]
+        z_words = [[kept([P, widths[b]], U32, "z_words%d_%d" % (b, c)) for c in range(T2 // widths[b])] for b in range(BLOCKS)]
+        z_plane = [[kept([P, widths[b]], U8, "z_plane%d_%d" % (b, c)) for c in range(T2 // widths[b])] for b in range(BLOCKS)]
+        ident = kept([P, P], F32, "ident")
+
+        bank_h1 = [psum.tile([P, HALF], F32, name="bank_h1_%d" % i) for i in range(2)]
+        bank_w2 = [psum.tile([P, HALF], F32, name="bank_w2_%d" % i) for i in range(2)]
+        bank_w3 = psum.tile([P, HALF], F32, name="bank_w3")
+        bank_back = [psum.tile([P, HALF], F32, name="bank_back%d" % i) for i in range(3)]
+
+        raw = {}
+        codes = {}
+        bg_sb = {}
+        turned = {}
+
+        def clear(tile_ap):
+            nc.vector.memset(tile_ap.bitcast(I32), 0)
+
+        def load_words(i, words, a):
+            nc.sync.dma_start(table[i][a][:], words[a].rearrange("p t i -> p (t i)").bitcast(I32))
+
+        def load_plane_rows(plane, scales):
+            for quad in range(4):
+                nc.sync.dma_start(
+                    plane[32 * quad : 32 * quad + 4],
+                    scales[:, 4 * quad : 4 * quad + 4, :].bitcast(I32).rearrange("a r c -> r a c"),
+                )
+
+        def load_weight(name, w, chunk):
+            for a in range(PASSES):
+                tile = raw_pool.tile([P, PACK, CHUNK], F32, name="raw_" + name, tag="raw_" + name)
+                rows = w[a * K_PASS : (a + 1) * K_PASS, chunk * CHUNK : (chunk + 1) * CHUNK]
+                nc.sync.dma_start(tile[:], rows.rearrange("(p j) c -> p j c", j=PACK))
+                raw[name, chunk, a] = tile
+
+        def load_bg(b):
+            for u in range(2):
+                tile = kept([P, 2, T2], F32, "bg%d_%d" % (b, u), "bg%d" % u)
+                rows = bg[b * K_PASS : (b + 1) * K_PASS, :].rearrange("(p t) m -> p t m", t=PACK)
+                nc.sync.dma_start(tile[:], rows[:, 2 * u : 2 * u + 2, :])
+                bg_sb[b, u] = tile
+
+        def quantise_weights(parts, tag):
+            label = "_".join("%s%d" % part for part in parts)
+            count = len(parts) * PASSES
+            grouped = stage[tag][:, : count * P * PACK].rearrange("p (n c j) -> p n c j", n=count, j=PACK)
+            for n, (name, s) in enumerate(parts):
+                for a in range(PASSES):
+                    nc.scalar.copy(
+                        grouped[:, n * PASSES + a].rearrange("p (c i) j -> p c j i", i=4),
+                        raw[name, s // 2, a][:, :, (s % 2) * P : (s % 2 + 1) * P].rearrange("p j (c i) -> p c j i", i=4),
+                    )
+            words = kept([P, count, P], U32, "words" + label)
+            plane = kept([P, count, P], U8, "plane" + label)
+            nc.vector.quantize_mx(
+                words[:].rearrange("p a c -> p (a c)").bitcast(FP8X4),
+                plane[:].rearrange("p a c -> p (a c)"),
+                stage[tag][:, : count * P * PACK],
+            )
+            for n, part in enumerate(parts):
+                codes[part] = (words, plane, n * PASSES)
+
+        def gather(dst, window, i):
+            nc.vector.tensor_copy(dst[:], window.indirect(idx[i][:]))
+
+        def product(bank, name, s, i, planes):
+            words, plane, first = codes[name, s]
+            for a in range(PASSES):
+                nc.tensor.matmul_mx(
+                    bank[:], words[:, first + a, :].bitcast(FP8X4), plane[:, first + a, :],
+                    v_words[i][a][:].bitcast(FP8X4), planes[a], start=a == 0, stop=a == PASSES - 1,
+                )
+
+        def trail_features(s):
+            product(bank_h1[s % 2], "w1", s, 0, [v_plane[4 * a :, :] for a in range(PASSES)])
+            nc.scalar.activation(h1_sb[s % 3][:], bank_h1[s % 2][:], ACT.Tanh)
+
+        def radiant_sums(s):
+            for a in range(PASSES):
+                nc.tensor.matmul_mx(
+                    bank_w2[s % 2][:], w2_sb[:, a, 2 * P * s : 2 * P * (s + 1)].bitcast(FP4X4),
+                    w2_plane[:, a, P * s : P * (s + 1)], v_words[1][a][:].bitcast(FP8X4), v2_plane[a][:],
+                    start=a == 0, stop=a == PASSES - 1,
+                )
+            product(bank_w3, "w3", s, 1, [v2_plane[a][:] for a in range(PASSES)])
+            nc.scalar.copy(sum2_sb[s % 2][:], bank_w2[s % 2][:])
+
+        def place_trails(s):
+            nc.vector.tensor_tensor(page_a[s % 3][:].indirect(idx[2][:]), h1_sb[s % 3][:], wg_sb[0][:], ALU.mult)
+
+        def place_radiants(s):
+            h2 = stage[s % 2][:, : 2 * S].bitcast(F32)
+            nc.vector.tensor_tensor(h2, bank_w3[:], sum2_sb[s % 2][:], ALU.max)
+            nc.vector.tensor_tensor(page_b[s % 2][:].indirect(idx[3][:]), h2, wg_sb[1][:], ALU.mult)
+
+        def add_turned(bank, first, second):
+            for g in range(4):
+                cols = bank[:, g * P : (g + 1) * P]
+                nc.tensor.matmul(cols, first(g), ident[:], start=True, stop=False, is_transpose=True)
+                nc.tensor.matmul(cols, second(g), ident[:], start=False, stop=True, is_transpose=True)
+
+        def join_pages(s):
+            b, part = divmod(s, 4)
+            if part == 0:
+                for kind in range(2):
+                    for h in range(HALVES):
+                        tag = "big%d" % (2 * kind + h) if b == 1 else None
+                        turned[b, kind, h] = kept([P, 4, PACK, P], F32, "turned%d_%d_%d" % (b, kind, h), tag)
+            banks = [bank_h1[s % 2], bank_w2[(s + 1) % 2]]
+            for h in range(HALVES):
+                add_turned(
+                    banks[h],
+                    lambda g: page_a[s % 3][:, h * HALF + g * P : h * HALF + (g + 1) * P],
+                    lambda g: page_b[s % 2][:, h * HALF + g * P : h * HALF + (g + 1) * P],
+                )
+            for h in range(HALVES):
+                q_t = banks[h][:].rearrange("m (g p t) -> m g t p", g=4, t=PACK)
+                rows = slice(32 * part, 32 * (part + 1))
+                nc.scalar.activation(turned[b, 0, h][:, :, :, rows], q_t, ACT.Silu, scale=-2.0)
+                if s == SLICES - 1:
+                    nc.vector.tensor_copy(turned[b, 1, h][:, :, :, rows], q_t)
+                else:
+                    nc.scalar.copy(turned[b, 1, h][:, :, :, rows], q_t)
+
+        def make_z_rows(b, c, ts, bank):
+            groups = widths[b] // P
+            h, g0 = divmod(c * groups, 4)
+            add_turned(
+                bank,
+                lambda g: turned[b, 0, h][:, g0 + g % groups, ts[g // groups], :],
+                lambda g: turned[b, 1, h][:, g0 + g % groups, ts[g // groups], :],
+            )
+            for e, t in enumerate(ts):
+                nc.vector.scalar_tensor_tensor(
+                    z_rows[b][c][:, t, :], bank[:, e * widths[b] : (e + 1) * widths[b]], gain_sb[:, b, t : t + 1],
+                    bg_sb[b, t // 2][:, t % 2, c * widths[b] : (c + 1) * widths[b]], ALU.mult, ALU.add,
+                )
+
+        def quantise_z(b, c):
+            grouped = ring.tile([P, widths[b], PACK], BF16, name="z_grouped", tag="z_grouped", align_bytes=64)
+            nc.scalar.copy(
+                grouped[:].rearrange("p (c i) t -> p c t i", i=4),
+                z_rows[b][c][:].rearrange("p t (c i) -> p c t i", i=4),
+            )
+            nc.vector.quantize_mx(
+                z_words[b][c][:].bitcast(FP8X4), z_plane[b][c][:], grouped[:].rearrange("p m t -> p (m t)")
+            )
+
+        def project(c, banks):
+            for pair in range(2):
+                bank = banks[pair]
+                for e in range(2):
+                    nt = 2 * pair + e
+                    for b in range(BLOCKS):
+                        piece, m0 = divmod(c * QUARTER, widths[b])
+                        nc.tensor.matmul_mx(
+                            bank[:, e * QUARTER : (e + 1) * QUARTER], w4_sb[:, b, 2 * P * nt : 2 * P * (nt + 1)].bitcast(FP4X4),
+                            w4_plane[:, b, P * nt : P * (nt + 1)], z_words[b][piece][:, m0 : m0 + QUARTER].bitcast(FP8X4),
+                            z_plane[b][piece][:, m0 : m0 + QUARTER],
+                            start=b == 0, stop=b == BLOCKS - 1,
+                        )
+                res = out_pool.tile([P, 2, QUARTER], F32, name="res")
+                if pair == 0:
+                    nc.scalar.copy(res[:].rearrange("p e m -> p (e m)"), bank[:])
+                else:
+                    nc.vector.tensor_copy(res[:].rearrange("p e m -> p (e m)"), bank[:])
+                rows = out[2 * pair * P : 2 * (pair + 1) * P, c * QUARTER : (c + 1) * QUARTER]
+                nc.sync.dma_start(rows.rearrange("(e p) m -> p e m", e=2), res[:])
+
+        clear(tab_plane[:])
+        clear(tab2_plane[:])
+        clear(page_a[0][:])
+        clear(page_a[1][:])
+        for tile in (w2_plane, page_a[2], page_b[0], page_b[1], w4_plane):
+            nc.gpsimd.memset(tile[:].bitcast(I32), 0)
+        make_identity(nc, ident[:])
+
+        for tile, offsets in zip(idx, (offs, offs2, offs3, offs4)):
+            nc.sync.dma_start(tile[:], offsets)
+        load_words(0, tab_words, 0)
+        load_weight("w1", w1, 0)
+        load_words(0, tab_words, 1)
+        for quad in range(4):
+            nc.scalar.dma_start(
+                tab_plane[32 * quad : 32 * quad + 4 * PASSES, :].bitcast(I32),
+                tab_scales[:, 4 * quad : 4 * quad + 4, :].bitcast(I32),
+            )
+        nc.sync.dma_start(wg_sb[0][:], wg1)
+        load_plane_rows(tab2_plane[:].bitcast(I32).rearrange("p (a t) -> p a t", a=PASSES), tab2_scales)
+        load_words(1, tab2_words, 0)
+        load_weight("w3", w3, 0)
+        load_plane_rows(w2_plane[:].bitcast(I32), w2_scales)
+        nc.sync.dma_start(w2_sb[:].bitcast(I32), w2_words.bitcast(I32).rearrange("a p c -> p a c"))
+        load_weight("w1", w1, 1)
+        load_words(1, tab2_words, 1)
+        nc.sync.dma_start(wg_sb[1][:], wg2)
+        load_weight("w3", w3, 1)
+        nc.sync.dma_start(gain_sb[:], gain.rearrange("(b p t) -> p b t", b=BLOCKS, t=PACK))
+        load_bg(0)
+        load_plane_rows(w4_plane[:].bitcast(I32), w4_scales)
+        nc.sync.dma_start(w4_sb[:].bitcast(I32), w4_words.bitcast(I32).rearrange("a p c -> p a c"))
+        for chunk in range(2, CHUNKS):
+            load_weight("w1", w1, chunk)
+            load_weight("w3", w3, chunk)
+
+        def step_parts(s):
+            return [("w1", s + 2)] * (s + 2 < SLICES) + [("w3", s + 1)] * (s + 1 < SLICES)
+
+        gather(v_words[0][0], table[0][0][:].bitcast(U32), 0)
+        gather(v_plane, tab_plane[:], 0)
+        quantise_weights([("w1", 0), ("w1", 1)], 1)
+        gather(v_words[0][1], table[0][1][:].bitcast(U32), 0)
+        for s in range(2):
+            trail_features(s)
+            place_trails(s)
+        for a in range(PASSES):
+            gather(v2_plane[a], tab2_plane[:, a * T : (a + 1) * T], 1)
+        quantise_weights([("w3", 0)], 2)
+        for a in range(PASSES):
+            gather(v_words[1][a], table[1][a][:].bitcast(U32), 1)
+        radiant_sums(0)
+        quantise_weights(step_parts(0), 0)
+        trail_features(2)
+        first_block = [(h, t) for t in range(PACK) for h in range(HALVES)]
+        for s in range(SLICES):
+            place_radiants(s)
+            if s + 2 < SLICES:
+                place_trails(s + 2)
+            if s + 1 < SLICES:
+                radiant_sums(s + 1)
+            if s + 2 < SLICES:
+                quantise_weights(step_parts(s + 1), (s + 1) % 2)
+            join_pages(s)
+            if s in (3, 4):
+                banks = [bank_h1[s % 2], bank_w2[(s + 1) % 2]]
+                banks = bank_back + banks if s == 3 else banks + bank_back[:1]
+                for bank in banks:
+                    h, t = first_block[0]
+                    first_block.remove((h, t))
+                    make_z_rows(0, h, [t], bank)
+            if s + 3 < SLICES:
+                trail_features(s + 3)
+            if s == 4:
+                load_bg(1)
+            if s in (5, 6):
+                quantise_z(0, s - 5)
+        spent = ["tab_plane", "tab2_plane", None, None]
+        z_rows.append([kept([P, PACK, QUARTER], BF16, "z_rows1_%d" % c, spent[c]) for c in range(QUARTERS)])
+        back = bank_back + [bank_h1[0]]
+        for c in range(QUARTERS + 1):
+            if c < QUARTERS:
+                for u in range(2):
+                    make_z_rows(1, c, [2 * u, 2 * u + 1], back[(2 * c + u) % 4])
+                quantise_z(1, c)
+            if c >= 1:
+                project(c - 1, [bank_w3, bank_w2[1]] if c % 2 else [bank_h1[1], bank_w2[0]])

@@ -40,8 +40,8 @@ def tile_list_meteor_catalogue_scores_kernel(
         lists = ctx.enter_context(tc.tile_pool(name="lists", bufs=1))
         keep = ctx.enter_context(tc.tile_pool(name="keep", bufs=1))
         raw_pool = ctx.enter_context(tc.tile_pool(name="raw", bufs=4))
+        stage_pool = ctx.enter_context(tc.tile_pool(name="stage", bufs=3))
         ring = ctx.enter_context(tc.tile_pool(name="ring", bufs=2))
-        out_pool = ctx.enter_context(tc.tile_pool(name="outs", bufs=3))
         psum = ctx.enter_context(tc.psum_pool(name="psum", bufs=1))
 
         def kept(shape, dtype, name, tag=None):
@@ -54,7 +54,7 @@ def tile_list_meteor_catalogue_scores_kernel(
         v_words = [[kept([P, S], U32, "v%d_%d" % (i, a)) for a in range(PASSES)] for i in range(2)]
         v_plane = kept([P, S], U8, "v_plane")
         v2_plane = [kept([P, S], U8, "v2_plane%d" % a) for a in range(PASSES)]
-        w2_sb = kept([P, PASSES, 2 * H], U8, "w2_sb")
+        w2_sb = [kept([P, PASSES, 2 * K_PASS], U8, "w2_sb%d" % b) for b in range(BLOCKS)]
         w2_plane = kept([P, PASSES, H], U8, "w2_plane")
         w4_sb = kept([P, BLOCKS, 2 * N], U8, "w4_sb")
         w4_plane = kept([P, BLOCKS, N], U8, "w4_plane")
@@ -64,11 +64,10 @@ def tile_list_meteor_catalogue_scores_kernel(
         page_b = [kept([P, T2], F32, "page_b%d" % i) for i in range(2)]
         h1_sb = [kept([P, S], F32, "h1_%d" % i) for i in range(3)]
         sum2_sb = [kept([P, S], F32, "sum2_%d" % i) for i in range(2)]
-        stage = [kept([P, 2 * PASSES * P * PACK], BF16, "stage%d" % i) for i in range(2)]
-        stage.append(kept([P, PASSES * P * PACK], BF16, "stage2"))
+        w2_dealt_plane = kept([P, PASSES, K_PASS], U8, "w2_dealt_plane")
         widths = [HALF, QUARTER]
         z_rows = [[kept([P, PACK, HALF], BF16, "z_rows0_%d" % h) for h in range(HALVES)]]
-        z_words = [[kept([P, widths[b]], U32, "z_words%d_%d" % (b, c)) for c in range(T2 // widths[b])] for b in range(BLOCKS)]
+        z_words = [[kept([P, HALF], U32, "z_words0_%d" % h) for h in range(HALVES)]]
         z_plane = [[kept([P, widths[b]], U8, "z_plane%d_%d" % (b, c)) for c in range(T2 // widths[b])] for b in range(BLOCKS)]
         ident = kept([P, P], F32, "ident")
 
@@ -81,6 +80,8 @@ def tile_list_meteor_catalogue_scores_kernel(
         codes = {}
         bg_sb = {}
         turned = {}
+        wg_dealt = []
+        dealt = []
 
         def clear(tile_ap):
             nc.vector.memset(tile_ap.bitcast(I32), 0)
@@ -95,48 +96,67 @@ def tile_list_meteor_catalogue_scores_kernel(
                     scales[:, 4 * quad : 4 * quad + 4, :].bitcast(I32).rearrange("a r c -> r a c"),
                 )
 
-        def load_weight(name, w, chunk):
+        def load_weight(name, w, c0, width, tiles):
             for a in range(PASSES):
-                tile = raw_pool.tile([P, PACK, CHUNK], F32, name="raw_" + name, tag="raw_" + name)
-                rows = w[a * K_PASS : (a + 1) * K_PASS, chunk * CHUNK : (chunk + 1) * CHUNK]
-                nc.sync.dma_start(tile[:], rows.rearrange("(p j) c -> p j c", j=PACK))
-                raw[name, chunk, a] = tile
+                rows = w[a * K_PASS : (a + 1) * K_PASS, c0 : c0 + width]
+                nc.sync.dma_start(tiles[a][:], rows.rearrange("(p j) c -> p j c", j=PACK))
+                raw[name, c0, a] = tiles[a]
 
-        def load_bg(b):
-            for u in range(2):
-                tile = kept([P, 2, T2], F32, "bg%d_%d" % (b, u), "bg%d" % u)
-                rows = bg[b * K_PASS : (b + 1) * K_PASS, :].rearrange("(p t) m -> p t m", t=PACK)
-                nc.sync.dma_start(tile[:], rows[:, 2 * u : 2 * u + 2, :])
-                bg_sb[b, u] = tile
+        def load_chunk(name, w, chunk, tag):
+            tiles = [raw_pool.tile([P, PACK, CHUNK], F32, name="raw_%s_%d" % (name, chunk), tag=tag) for a in range(PASSES)]
+            load_weight(name, w, chunk * CHUNK, CHUNK, tiles)
 
-        def quantise_weights(parts, tag):
-            label = "_".join("%s%d" % part for part in parts)
-            count = len(parts) * PASSES
-            grouped = stage[tag][:, : count * P * PACK].rearrange("p (n c j) -> p n c j", n=count, j=PACK)
-            for n, (name, s) in enumerate(parts):
-                for a in range(PASSES):
+        def load_w2(b):
+            words = w2_words[:, :, 2 * K_PASS * b : 2 * K_PASS * (b + 1)]
+            nc.sync.dma_start(w2_sb[b][:].bitcast(I32), words.bitcast(I32).rearrange("a p c -> p a c"))
+
+        def load_bg(b, u, tag):
+            rows = bg[b * K_PASS : (b + 1) * K_PASS, :].rearrange("(p t) m -> p t m", t=PACK)
+            tile = kept([P, 2, T2], F32, "bg%d_%d" % (b, u), tag)
+            nc.sync.dma_start(tile[:], rows[:, 2 * u : 2 * u + 2, :])
+            for e in range(2):
+                bg_sb[b, 2 * u + e] = tile[:, e, :]
+
+        def load_dealt_gates(i, wg):
+            tile = kept([P, PACK, S], F32, "wg_dealt%d" % i, "big%d" % (2 + i))
+            for quad in range(4):
+                nc.sync.dma_start(tile[32 * quad : 32 * (quad + 1)], wg.rearrange("(q t) j -> q t j", t=PACK))
+            wg_dealt.append(tile)
+
+        def quantise_weight(name, pair):
+            grouped = stage_pool.tile([P, PASSES, CHUNK, PACK], BF16, name="grouped", tag="stage", align_bytes=64)
+            for a in range(PASSES):
+                if pair < 2:
                     nc.scalar.copy(
-                        grouped[:, n * PASSES + a].rearrange("p (c i) j -> p c j i", i=4),
-                        raw[name, s // 2, a][:, :, (s % 2) * P : (s % 2 + 1) * P].rearrange("p j (c i) -> p c j i", i=4),
+                        grouped[:, a].rearrange("p (c i) j -> p c j i", i=4),
+                        raw[name, pair * CHUNK, a][:].rearrange("p j (c i) -> p c j i", i=4),
                     )
-            words = kept([P, count, P], U32, "words" + label)
-            plane = kept([P, count, P], U8, "plane" + label)
+                    continue
+                for c0 in [c0 for (other, c0, b) in raw if other == name and b == a and c0 >= K_PASS]:
+                    source = raw[name, c0, a][:].rearrange("p j (q t) -> p q j t", t=PACK)
+                    q0 = (c0 - K_PASS) // PACK
+                    nc.scalar.copy(
+                        grouped[:, a].rearrange("p (e q) j -> p q j e", e=2)[:, q0 : q0 + source.shape[1]],
+                        source[:, :, :, 2 * (pair - 2) : 2 * (pair - 1)],
+                    )
+            words = kept([P, PASSES, CHUNK], U32, "words_%s_%d" % (name, pair))
+            plane = kept([P, PASSES, CHUNK], U8, "plane_%s_%d" % (name, pair))
             nc.vector.quantize_mx(
                 words[:].rearrange("p a c -> p (a c)").bitcast(FP8X4),
                 plane[:].rearrange("p a c -> p (a c)"),
-                stage[tag][:, : count * P * PACK],
+                grouped[:].rearrange("p a c j -> p (a c j)"),
             )
-            for n, part in enumerate(parts):
-                codes[part] = (words, plane, n * PASSES)
+            for e in range(2):
+                codes[name, 2 * pair + e] = (words, plane, e * P)
 
         def gather(dst, window, i):
             nc.vector.tensor_copy(dst[:], window.indirect(idx[i][:]))
 
         def product(bank, name, s, i, planes):
-            words, plane, first = codes[name, s]
+            words, plane, c0 = codes[name, s]
             for a in range(PASSES):
                 nc.tensor.matmul_mx(
-                    bank[:], words[:, first + a, :].bitcast(FP8X4), plane[:, first + a, :],
+                    bank[:], words[:, a, c0 : c0 + P].bitcast(FP8X4), plane[:, a, c0 : c0 + P],
                     v_words[i][a][:].bitcast(FP8X4), planes[a], start=a == 0, stop=a == PASSES - 1,
                 )
 
@@ -144,23 +164,43 @@ def tile_list_meteor_catalogue_scores_kernel(
             product(bank_h1[s % 2], "w1", s, 0, [v_plane[4 * a :, :] for a in range(PASSES)])
             nc.scalar.activation(h1_sb[s % 3][:], bank_h1[s % 2][:], ACT.Tanh)
 
+        def deal_w2():
+            w2_dealt = kept([P, PASSES, 2 * K_PASS], U8, "w2_dealt", "tab_plane")
+            dealt.append(w2_dealt)
+            nc.vector.tensor_copy(
+                w2_dealt[:].bitcast(U16).rearrange("p a (t q) -> p a q t", t=PACK),
+                w2_sb[1][:].bitcast(U16).rearrange("p a (q t) -> p a q t", t=PACK),
+            )
+            nc.vector.tensor_copy(
+                w2_dealt_plane[:].rearrange("p a (t q) -> p a q t", t=PACK),
+                w2_plane[:, :, K_PASS:].rearrange("p a (q t) -> p a q t", t=PACK),
+            )
+
         def radiant_sums(s):
+            words, plane = (w2_sb[0], w2_plane) if s < 4 else (dealt[0], w2_dealt_plane)
+            c0 = P * (s % 4)
             for a in range(PASSES):
                 nc.tensor.matmul_mx(
-                    bank_w2[s % 2][:], w2_sb[:, a, 2 * P * s : 2 * P * (s + 1)].bitcast(FP4X4),
-                    w2_plane[:, a, P * s : P * (s + 1)], v_words[1][a][:].bitcast(FP8X4), v2_plane[a][:],
-                    start=a == 0, stop=a == PASSES - 1,
+                    bank_w2[s % 2][:], words[:, a, 2 * c0 : 2 * (c0 + P)].bitcast(FP4X4), plane[:, a, c0 : c0 + P],
+                    v_words[1][a][:].bitcast(FP8X4), v2_plane[a][:], start=a == 0, stop=a == PASSES - 1,
                 )
             product(bank_w3, "w3", s, 1, [v2_plane[a][:] for a in range(PASSES)])
             nc.scalar.copy(sum2_sb[s % 2][:], bank_w2[s % 2][:])
 
+        def gates(i, s):
+            return wg_sb[i][:] if s < 4 else wg_dealt[i][:, s - 4, :]
+
         def place_trails(s):
-            nc.vector.tensor_tensor(page_a[s % 3][:].indirect(idx[2][:]), h1_sb[s % 3][:], wg_sb[0][:], ALU.mult)
+            nc.vector.tensor_tensor(page_a[s % 3][:].indirect(idx[2][:]), h1_sb[s % 3][:], gates(0, s), ALU.mult)
 
         def place_radiants(s):
-            h2 = stage[s % 2][:, : 2 * S].bitcast(F32)
+            spent = {5: (0, 1), 6: (0, 3), 7: (1, 1)}
+            if s in spent:
+                h2 = bg_sb[spent[s]][:, HALF:]
+            else:
+                h2 = sum2_sb[s % 2][:]
             nc.vector.tensor_tensor(h2, bank_w3[:], sum2_sb[s % 2][:], ALU.max)
-            nc.vector.tensor_tensor(page_b[s % 2][:].indirect(idx[3][:]), h2, wg_sb[1][:], ALU.mult)
+            nc.vector.tensor_tensor(page_b[s % 2][:].indirect(idx[3][:]), h2, gates(1, s), ALU.mult)
 
         def add_turned(bank, first, second):
             for g in range(4):
@@ -169,12 +209,6 @@ def tile_list_meteor_catalogue_scores_kernel(
                 nc.tensor.matmul(cols, second(g), ident[:], start=False, stop=True, is_transpose=True)
 
         def join_pages(s):
-            b, part = divmod(s, 4)
-            if part == 0:
-                for kind in range(2):
-                    for h in range(HALVES):
-                        tag = "big%d" % (2 * kind + h) if b == 1 else None
-                        turned[b, kind, h] = kept([P, 4, PACK, P], F32, "turned%d_%d_%d" % (b, kind, h), tag)
             banks = [bank_h1[s % 2], bank_w2[(s + 1) % 2]]
             for h in range(HALVES):
                 add_turned(
@@ -182,59 +216,82 @@ def tile_list_meteor_catalogue_scores_kernel(
                     lambda g: page_a[s % 3][:, h * HALF + g * P : h * HALF + (g + 1) * P],
                     lambda g: page_b[s % 2][:, h * HALF + g * P : h * HALF + (g + 1) * P],
                 )
+            if s < 4:
+                for h in range(HALVES):
+                    q_t = banks[h][:].rearrange("m (g p t) -> m g t p", g=4, t=PACK)
+                    rows = slice(32 * s, 32 * (s + 1))
+                    nc.scalar.activation(turned[0, h][:, :, :, rows], q_t, ACT.Silu, scale=-2.0)
+                    nc.scalar.copy(turned[1, h][:, :, :, rows], q_t)
+                return
+            both = [raw_pool.tile([P, T2], F32, name="turned%d_%d" % (s, kind), tag="raw_w3") for kind in range(2)]
             for h in range(HALVES):
-                q_t = banks[h][:].rearrange("m (g p t) -> m g t p", g=4, t=PACK)
-                rows = slice(32 * part, 32 * (part + 1))
-                nc.scalar.activation(turned[b, 0, h][:, :, :, rows], q_t, ACT.Silu, scale=-2.0)
-                if s == SLICES - 1:
-                    nc.vector.tensor_copy(turned[b, 1, h][:, :, :, rows], q_t)
-                else:
-                    nc.scalar.copy(turned[b, 1, h][:, :, :, rows], q_t)
+                cols = slice(h * HALF, (h + 1) * HALF)
+                nc.scalar.activation(both[0][:, cols], banks[h][:], ACT.Silu, scale=-2.0)
+                nc.scalar.copy(both[1][:, cols], banks[h][:])
+            turned[s] = both
 
-        def make_z_rows(b, c, ts, bank):
-            groups = widths[b] // P
-            h, g0 = divmod(c * groups, 4)
-            add_turned(
-                bank,
-                lambda g: turned[b, 0, h][:, g0 + g % groups, ts[g // groups], :],
-                lambda g: turned[b, 1, h][:, g0 + g % groups, ts[g // groups], :],
-            )
-            for e, t in enumerate(ts):
-                nc.vector.scalar_tensor_tensor(
-                    z_rows[b][c][:, t, :], bank[:, e * widths[b] : (e + 1) * widths[b]], gain_sb[:, b, t : t + 1],
-                    bg_sb[b, t // 2][:, t % 2, c * widths[b] : (c + 1) * widths[b]], ALU.mult, ALU.add,
+        def turn_back(s):
+            both = turned[s]
+            for h in range(HALVES):
+                bank = back_banks[s][h]
+                add_turned(
+                    bank,
+                    lambda g: both[0][:, h * HALF + g * P : h * HALF + (g + 1) * P],
+                    lambda g: both[1][:, h * HALF + g * P : h * HALF + (g + 1) * P],
                 )
+                finish_z(1, h, s - 4, bank[:], bg_sb[1, s - 4][:, h * HALF : (h + 1) * HALF])
+
+        def finish_z(b, h, t, values, addend):
+            nc.vector.scalar_tensor_tensor(z_rows[b][h][:, t, :], values, gain_sb[:, b, t : t + 1], addend, ALU.mult, ALU.add)
+
+        def make_z_rows(h, t, bank):
+            add_turned(bank, lambda g: turned[0, h][:, g, t, :], lambda g: turned[1, h][:, g, t, :])
+            finish_z(0, h, t, bank[:], bg_sb[0, t][:, h * HALF : (h + 1) * HALF])
+
+        def last_z_rows():
+            s, t = SLICES - 1, PACK - 1
+            q, part, curve = [
+                [kept([P, HALF], F32, "last%d_%d" % (kind, h), ("turned0_%d", "turned1_%d", "big%d")[kind] % h) for h in range(HALVES)]
+                for kind in range(3)
+            ]
+            for h in range(HALVES):
+                cols = slice(h * HALF, (h + 1) * HALF)
+                nc.vector.tensor_tensor(q[h][:], page_a[s % 3][:, cols], page_b[s % 2][:, cols], ALU.add)
+                nc.scalar.activation(curve[h][:], q[h][:], ACT.Silu, scale=-2.0)
+            for h in range(HALVES):
+                cols = slice(h * HALF, (h + 1) * HALF)
+                nc.vector.scalar_tensor_tensor(part[h][:], q[h][:], gain_sb[:, 1, t : t + 1], bg_sb[1, t][:, cols], ALU.mult, ALU.add)
+                finish_z(1, h, t, curve[h][:], part[h][:])
 
         def quantise_z(b, c):
+            h, m0 = divmod(c * widths[b], HALF)
             grouped = ring.tile([P, widths[b], PACK], BF16, name="z_grouped", tag="z_grouped", align_bytes=64)
-            nc.scalar.copy(
+            move = nc.vector.tensor_copy if b == 1 and c % 2 == 1 else nc.scalar.copy
+            move(
                 grouped[:].rearrange("p (c i) t -> p c t i", i=4),
-                z_rows[b][c][:].rearrange("p t (c i) -> p c t i", i=4),
+                z_rows[b][h][:, :, m0 : m0 + widths[b]].rearrange("p t (c i) -> p c t i", i=4),
             )
             nc.vector.quantize_mx(
                 z_words[b][c][:].bitcast(FP8X4), z_plane[b][c][:], grouped[:].rearrange("p m t -> p (m t)")
             )
 
-        def project(c, banks):
-            for pair in range(2):
-                bank = banks[pair]
-                for e in range(2):
-                    nt = 2 * pair + e
-                    for b in range(BLOCKS):
-                        piece, m0 = divmod(c * QUARTER, widths[b])
-                        nc.tensor.matmul_mx(
-                            bank[:, e * QUARTER : (e + 1) * QUARTER], w4_sb[:, b, 2 * P * nt : 2 * P * (nt + 1)].bitcast(FP4X4),
-                            w4_plane[:, b, P * nt : P * (nt + 1)], z_words[b][piece][:, m0 : m0 + QUARTER].bitcast(FP8X4),
-                            z_plane[b][piece][:, m0 : m0 + QUARTER],
-                            start=b == 0, stop=b == BLOCKS - 1,
-                        )
-                res = out_pool.tile([P, 2, QUARTER], F32, name="res")
-                if pair == 0:
-                    nc.scalar.copy(res[:].rearrange("p e m -> p (e m)"), bank[:])
+        def project(b, c):
+            h, m0 = divmod(c * widths[b], HALF)
+            for nt in range(N // P):
+                nc.tensor.matmul_mx(
+                    out_banks[h * 4 + nt][:, m0 : m0 + widths[b]], w4_sb[:, b, 2 * P * nt : 2 * P * (nt + 1)].bitcast(FP4X4),
+                    w4_plane[:, b, P * nt : P * (nt + 1)], z_words[b][c][:].bitcast(FP8X4), z_plane[b][c][:],
+                    start=b == 0, stop=b == 1 and m0 > 0,
+                )
+
+        def store(h):
+            for nt in range(N // P):
+                res = kept([P, HALF], F32, "res%d_%d" % (h, nt), ("sum2_0", "sum2_1", "h1_0", "h1_1", "h1_2", "words_w1_0", "words_w1_1", "words_w1_2")[4 * h + nt])
+                if nt == 0:
+                    nc.vector.tensor_copy(res[:], out_banks[h * 4 + nt][:])
                 else:
-                    nc.vector.tensor_copy(res[:].rearrange("p e m -> p (e m)"), bank[:])
-                rows = out[2 * pair * P : 2 * (pair + 1) * P, c * QUARTER : (c + 1) * QUARTER]
-                nc.sync.dma_start(rows.rearrange("(e p) m -> p e m", e=2), res[:])
+                    nc.scalar.copy(res[:], out_banks[h * 4 + nt][:])
+                nc.sync.dma_start(out[nt * P : (nt + 1) * P, h * HALF : (h + 1) * HALF], res[:])
 
         clear(tab_plane[:])
         clear(tab2_plane[:])
@@ -246,80 +303,92 @@ def tile_list_meteor_catalogue_scores_kernel(
 
         for tile, offsets in zip(idx, (offs, offs2, offs3, offs4)):
             nc.sync.dma_start(tile[:], offsets)
+        nc.sync.dma_start(gain_sb[:], gain.rearrange("(b p t) -> p b t", b=BLOCKS, t=PACK))
         load_words(0, tab_words, 0)
-        load_weight("w1", w1, 0)
-        load_words(0, tab_words, 1)
         for quad in range(4):
-            nc.scalar.dma_start(
+            nc.sync.dma_start(
                 tab_plane[32 * quad : 32 * quad + 4 * PASSES, :].bitcast(I32),
                 tab_scales[:, 4 * quad : 4 * quad + 4, :].bitcast(I32),
             )
-        nc.sync.dma_start(wg_sb[0][:], wg1)
+        load_chunk("w1", w1, 0, "raw_w1")
         load_plane_rows(tab2_plane[:].bitcast(I32).rearrange("p (a t) -> p a t", a=PASSES), tab2_scales)
+        load_chunk("w1", w1, 1, "raw_w1")
+        load_words(0, tab_words, 1)
+        nc.sync.dma_start(wg_sb[0][:], wg1)
+        load_chunk("w3", w3, 0, "raw_w3")
+        load_chunk("w3", w3, 1, "raw_w3")
         load_words(1, tab2_words, 0)
-        load_weight("w3", w3, 0)
+        load_weight("w1", w1, K_PASS, K_PASS, [kept([P, PACK, K_PASS], F32, "raw_w1_b%d" % a, "big%d" % a) for a in range(PASSES)])
         load_plane_rows(w2_plane[:].bitcast(I32), w2_scales)
-        nc.sync.dma_start(w2_sb[:].bitcast(I32), w2_words.bitcast(I32).rearrange("a p c -> p a c"))
-        load_weight("w1", w1, 1)
-        load_words(1, tab2_words, 1)
+        load_w2(0)
         nc.sync.dma_start(wg_sb[1][:], wg2)
-        load_weight("w3", w3, 1)
-        nc.sync.dma_start(gain_sb[:], gain.rearrange("(b p t) -> p b t", b=BLOCKS, t=PACK))
-        load_bg(0)
+        load_words(1, tab2_words, 1)
+        load_w2(1)
+        load_chunk("w3", w3, 2, "raw_w1")
+        load_chunk("w3", w3, 3, "raw_w1")
+        load_dealt_gates(0, wg1)
+        load_dealt_gates(1, wg2)
+        load_bg(0, 0, "bg_first")
+        load_bg(1, 0, None)
+        load_bg(1, 1, None)
         load_plane_rows(w4_plane[:].bitcast(I32), w4_scales)
         nc.sync.dma_start(w4_sb[:].bitcast(I32), w4_words.bitcast(I32).rearrange("a p c -> p a c"))
-        for chunk in range(2, CHUNKS):
-            load_weight("w1", w1, chunk)
-            load_weight("w3", w3, chunk)
 
-        def step_parts(s):
-            return [("w1", s + 2)] * (s + 2 < SLICES) + [("w3", s + 1)] * (s + 1 < SLICES)
-
+        for kind in range(2):
+            for h in range(HALVES):
+                turned[kind, h] = kept([P, 4, PACK, P], F32, "turned%d_%d" % (kind, h))
         gather(v_words[0][0], table[0][0][:].bitcast(U32), 0)
         gather(v_plane, tab_plane[:], 0)
-        quantise_weights([("w1", 0), ("w1", 1)], 1)
+        quantise_weight("w1", 0)
         gather(v_words[0][1], table[0][1][:].bitcast(U32), 0)
         for s in range(2):
             trail_features(s)
             place_trails(s)
         for a in range(PASSES):
             gather(v2_plane[a], tab2_plane[:, a * T : (a + 1) * T], 1)
-        quantise_weights([("w3", 0)], 2)
+        quantise_weight("w1", 1)
+        quantise_weight("w3", 0)
+        trail_features(2)
+        place_trails(2)
         for a in range(PASSES):
             gather(v_words[1][a], table[1][a][:].bitcast(U32), 1)
         radiant_sums(0)
-        quantise_weights(step_parts(0), 0)
-        trail_features(2)
-        first_block = [(h, t) for t in range(PACK) for h in range(HALVES)]
-        for s in range(SLICES):
+        deal_w2()
+        for name, pair in (("w3", 1), ("w1", 2), ("w1", 3), ("w3", 2), ("w3", 3)):
+            quantise_weight(name, pair)
+        z_rows.append([kept([P, PACK, HALF], BF16, "z_rows1_0", "tab2_plane"), stage_pool.tile([P, PACK, HALF], BF16, name="z_rows1_1", tag="stage", align_bytes=64)])
+        back_banks = {4: [bank_h1[0], bank_back[0]], 5: [bank_h1[1], bank_w2[0]], 6: [bank_h1[0], bank_w2[1]]}
+        for s in range(SLICES - 1):
             place_radiants(s)
-            if s + 2 < SLICES:
+            if 1 <= s < SLICES - 2:
                 place_trails(s + 2)
-            if s + 1 < SLICES:
-                radiant_sums(s + 1)
-            if s + 2 < SLICES:
-                quantise_weights(step_parts(s + 1), (s + 1) % 2)
-            join_pages(s)
-            if s in (3, 4):
-                banks = [bank_h1[s % 2], bank_w2[(s + 1) % 2]]
-                banks = bank_back + banks if s == 3 else banks + bank_back[:1]
-                for bank in banks:
-                    h, t = first_block[0]
-                    first_block.remove((h, t))
-                    make_z_rows(0, h, [t], bank)
+            radiant_sums(s + 1)
+            if s == 3:
+                join_pages(s)
+                for n, bank in enumerate(bank_back + [bank_h1[1]]):
+                    make_z_rows(n % 2, n // 2, bank)
+            elif s == 5:
+                load_bg(0, 1, "bg_first")
+                join_pages(s)
+                for n, bank in enumerate([bank_back[1], bank_back[2], bank_back[0], bank_h1[0]]):
+                    make_z_rows(n % 2, 2 + n // 2, bank)
+                for h in range(HALVES):
+                    quantise_z(0, h)
+            else:
+                join_pages(s)
+            if s >= 4:
+                turn_back(s)
             if s + 3 < SLICES:
                 trail_features(s + 3)
-            if s == 4:
-                load_bg(1)
-            if s in (5, 6):
-                quantise_z(0, s - 5)
-        spent = ["tab_plane", "tab2_plane", None, None]
-        z_rows.append([kept([P, PACK, QUARTER], BF16, "z_rows1_%d" % c, spent[c]) for c in range(QUARTERS)])
-        back = bank_back + [bank_h1[0]]
-        for c in range(QUARTERS + 1):
-            if c < QUARTERS:
-                for u in range(2):
-                    make_z_rows(1, c, [2 * u, 2 * u + 1], back[(2 * c + u) % 4])
-                quantise_z(1, c)
-            if c >= 1:
-                project(c - 1, [bank_w3, bank_w2[1]] if c % 2 else [bank_h1[1], bank_w2[0]])
+        place_radiants(SLICES - 1)
+        spent_words = ("words_w3_0", "words_w3_1", "words_w1_3", "words_w3_2")
+        z_words.append([kept([P, QUARTER], U32, "z_words1_%d" % c, spent_words[c]) for c in range(QUARTERS)])
+        out_banks = [bank_back[1], bank_back[2], bank_back[0], bank_h1[1], bank_w2[0], bank_w3, bank_h1[0], bank_w2[1]]
+        for h in range(HALVES):
+            project(0, h)
+        last_z_rows()
+        for c in range(QUARTERS):
+            quantise_z(1, c)
+            project(1, c)
+            if c % 2 == 1:
+                store(c // 2)

@@ -40,8 +40,7 @@ def tile_list_meteor_catalogue_scores_kernel(
         lists = ctx.enter_context(tc.tile_pool(name="lists", bufs=1))
         keep = ctx.enter_context(tc.tile_pool(name="keep", bufs=1))
         raw_pool = ctx.enter_context(tc.tile_pool(name="raw", bufs=4))
-        stage_pool = ctx.enter_context(tc.tile_pool(name="stage", bufs=3))
-        ring = ctx.enter_context(tc.tile_pool(name="ring", bufs=2))
+        stage_pool = ctx.enter_context(tc.tile_pool(name="stage", bufs=4))
         psum = ctx.enter_context(tc.psum_pool(name="psum", bufs=1))
 
         def kept(shape, dtype, name, tag=None):
@@ -82,6 +81,8 @@ def tile_list_meteor_catalogue_scores_kernel(
         turned = {}
         wg_dealt = []
         dealt = []
+        held = {("w1", 1): kept([P, PASSES, CHUNK, PACK], BF16, "held")}
+        h1_second = held["w1", 1][:].rearrange("p a c j -> p (a c j)")[:, : 2 * S].bitcast(F32)
 
         def clear(tile_ap):
             nc.vector.memset(tile_ap.bitcast(I32), 0)
@@ -124,7 +125,10 @@ def tile_list_meteor_catalogue_scores_kernel(
             wg_dealt.append(tile)
 
         def quantise_weight(name, pair):
-            grouped = stage_pool.tile([P, PASSES, CHUNK, PACK], BF16, name="grouped", tag="stage", align_bytes=64)
+            if (name, pair) in held:
+                grouped = held[name, pair]
+            else:
+                grouped = stage_pool.tile([P, PASSES, CHUNK, PACK], BF16, name="grouped", tag="stage", align_bytes=64)
             for a in range(PASSES):
                 if pair < 2:
                     nc.scalar.copy(
@@ -162,18 +166,18 @@ def tile_list_meteor_catalogue_scores_kernel(
 
         def trail_features(s):
             product(bank_h1[s % 2], "w1", s, 0, [v_plane[4 * a :, :] for a in range(PASSES)])
-            nc.scalar.activation(h1_sb[s % 3][:], bank_h1[s % 2][:], ACT.Tanh)
+            nc.scalar.activation(h1_second if s == 1 else h1_sb[s % 3][:], bank_h1[s % 2][:], ACT.Tanh)
 
         def deal_w2():
             w2_dealt = kept([P, PASSES, 2 * K_PASS], U8, "w2_dealt", "tab_plane")
             dealt.append(w2_dealt)
             nc.vector.tensor_copy(
-                w2_dealt[:].bitcast(U16).rearrange("p a (t q) -> p a q t", t=PACK),
-                w2_sb[1][:].bitcast(U16).rearrange("p a (q t) -> p a q t", t=PACK),
+                w2_dealt[:].bitcast(U16).rearrange("p a (t q) -> p a t q", t=PACK),
+                w2_sb[1][:].bitcast(U16).rearrange("p a (q t) -> p a t q", t=PACK),
             )
             nc.vector.tensor_copy(
-                w2_dealt_plane[:].rearrange("p a (t q) -> p a q t", t=PACK),
-                w2_plane[:, :, K_PASS:].rearrange("p a (q t) -> p a q t", t=PACK),
+                w2_dealt_plane[:].rearrange("p a (t q) -> p a t q", t=PACK),
+                w2_plane[:, :, K_PASS:].rearrange("p a (q t) -> p a t q", t=PACK),
             )
 
         def radiant_sums(s):
@@ -191,7 +195,7 @@ def tile_list_meteor_catalogue_scores_kernel(
             return wg_sb[i][:] if s < 4 else wg_dealt[i][:, s - 4, :]
 
         def place_trails(s):
-            nc.vector.tensor_tensor(page_a[s % 3][:].indirect(idx[2][:]), h1_sb[s % 3][:], gates(0, s), ALU.mult)
+            nc.vector.tensor_tensor(page_a[s % 3][:].indirect(idx[2][:]), h1_second if s == 1 else h1_sb[s % 3][:], gates(0, s), ALU.mult)
 
         def place_radiants(s):
             spent = {5: (0, 1), 6: (0, 3), 7: (1, 1)}
@@ -250,22 +254,24 @@ def tile_list_meteor_catalogue_scores_kernel(
 
         def last_z_rows():
             s, t = SLICES - 1, PACK - 1
-            q, part, curve = [
-                [kept([P, HALF], F32, "last%d_%d" % (kind, h), ("turned0_%d", "turned1_%d", "big%d")[kind] % h) for h in range(HALVES)]
-                for kind in range(3)
-            ]
-            for h in range(HALVES):
-                cols = slice(h * HALF, (h + 1) * HALF)
-                nc.vector.tensor_tensor(q[h][:], page_a[s % 3][:, cols], page_b[s % 2][:, cols], ALU.add)
-                nc.scalar.activation(curve[h][:], q[h][:], ACT.Silu, scale=-2.0)
-            for h in range(HALVES):
-                cols = slice(h * HALF, (h + 1) * HALF)
-                nc.vector.scalar_tensor_tensor(part[h][:], q[h][:], gain_sb[:, 1, t : t + 1], bg_sb[1, t][:, cols], ALU.mult, ALU.add)
-                finish_z(1, h, t, curve[h][:], part[h][:])
+            q, part, curve = [kept([P, T2], F32, "last%d" % kind, ("turned0_0", "turned1_0", "big1")[kind]) for kind in range(3)]
+            for cols in (slice(0, QUARTER), slice(QUARTER, T2)):
+                nc.vector.tensor_tensor(q[:, cols], page_a[s % 3][:, cols], page_b[s % 2][:, cols], ALU.add)
+                nc.scalar.activation(curve[:, cols], q[:, cols], ACT.Silu, scale=-2.0)
+            for c in range(QUARTERS):
+                cols = slice(c * QUARTER, (c + 1) * QUARTER)
+                h, m0 = divmod(c * QUARTER, HALF)
+                nc.vector.scalar_tensor_tensor(part[:, cols], q[:, cols], gain_sb[:, 1, t : t + 1], bg_sb[1, t][:, cols], ALU.mult, ALU.add)
+                nc.vector.scalar_tensor_tensor(
+                    z_rows[1][h][:, t, m0 : m0 + QUARTER], curve[:, cols], gain_sb[:, 1, t : t + 1], part[:, cols], ALU.mult, ALU.add
+                )
+                quantise_z(1, c)
+                project(1, c)
+                store(c)
 
         def quantise_z(b, c):
             h, m0 = divmod(c * widths[b], HALF)
-            grouped = ring.tile([P, widths[b], PACK], BF16, name="z_grouped", tag="z_grouped", align_bytes=64)
+            grouped = stage_pool.tile([P, widths[b], PACK], BF16, name="z_grouped", tag="stage", align_bytes=64)
             move = nc.vector.tensor_copy if b == 1 and c % 2 == 1 else nc.scalar.copy
             move(
                 grouped[:].rearrange("p (c i) t -> p c t i", i=4),
@@ -276,22 +282,24 @@ def tile_list_meteor_catalogue_scores_kernel(
             )
 
         def project(b, c):
-            h, m0 = divmod(c * widths[b], HALF)
+            piece, m0 = divmod(c * QUARTER, widths[b])
             for nt in range(N // P):
+                pair, e = divmod(nt, 2)
                 nc.tensor.matmul_mx(
-                    out_banks[h * 4 + nt][:, m0 : m0 + widths[b]], w4_sb[:, b, 2 * P * nt : 2 * P * (nt + 1)].bitcast(FP4X4),
-                    w4_plane[:, b, P * nt : P * (nt + 1)], z_words[b][c][:].bitcast(FP8X4), z_plane[b][c][:],
-                    start=b == 0, stop=b == 1 and m0 > 0,
+                    out_banks[2 * c + pair][:, e * QUARTER : (e + 1) * QUARTER],
+                    w4_sb[:, b, 2 * P * nt : 2 * P * (nt + 1)].bitcast(FP4X4), w4_plane[:, b, P * nt : P * (nt + 1)],
+                    z_words[b][piece][:, m0 : m0 + QUARTER].bitcast(FP8X4), z_plane[b][piece][:, m0 : m0 + QUARTER],
+                    start=b == 0 and e == 0, stop=b == 1 and e == 1,
                 )
 
-        def store(h):
-            for nt in range(N // P):
-                res = kept([P, HALF], F32, "res%d_%d" % (h, nt), ("sum2_0", "sum2_1", "h1_0", "h1_1", "h1_2", "words_w1_0", "words_w1_1", "words_w1_2")[4 * h + nt])
-                if nt == 0:
-                    nc.vector.tensor_copy(res[:], out_banks[h * 4 + nt][:])
-                else:
-                    nc.scalar.copy(res[:], out_banks[h * 4 + nt][:])
-                nc.sync.dma_start(out[nt * P : (nt + 1) * P, h * HALF : (h + 1) * HALF], res[:])
+        def store(c):
+            spent_tiles = ("sum2_0", "sum2_1", "h1_0", "h1_1", "h1_2", "words_w1_0", "words_w1_1", "words_w1_2")
+            for pair in range(2):
+                res = kept([P, 2, QUARTER], F32, "res%d_%d" % (c, pair), spent_tiles[2 * c + pair])
+                move = nc.vector.tensor_copy if c == 3 and pair == 0 else nc.scalar.copy
+                move(res[:].rearrange("p e m -> p (e m)"), out_banks[2 * c + pair][:])
+                rows = out[2 * pair * P : 2 * (pair + 1) * P, c * QUARTER : (c + 1) * QUARTER]
+                nc.sync.dma_start(rows.rearrange("(e p) m -> p e m", e=2), res[:])
 
         clear(tab_plane[:])
         clear(tab2_plane[:])
@@ -311,13 +319,13 @@ def tile_list_meteor_catalogue_scores_kernel(
                 tab_scales[:, 4 * quad : 4 * quad + 4, :].bitcast(I32),
             )
         load_chunk("w1", w1, 0, "raw_w1")
-        load_plane_rows(tab2_plane[:].bitcast(I32).rearrange("p (a t) -> p a t", a=PASSES), tab2_scales)
-        load_chunk("w1", w1, 1, "raw_w1")
         load_words(0, tab_words, 1)
         nc.sync.dma_start(wg_sb[0][:], wg1)
+        load_chunk("w1", w1, 1, "raw_w1")
+        load_words(1, tab2_words, 0)
+        load_plane_rows(tab2_plane[:].bitcast(I32).rearrange("p (a t) -> p a t", a=PASSES), tab2_scales)
         load_chunk("w3", w3, 0, "raw_w3")
         load_chunk("w3", w3, 1, "raw_w3")
-        load_words(1, tab2_words, 0)
         load_weight("w1", w1, K_PASS, K_PASS, [kept([P, PACK, K_PASS], F32, "raw_w1_b%d" % a, "big%d" % a) for a in range(PASSES)])
         load_plane_rows(w2_plane[:].bitcast(I32), w2_scales)
         load_w2(0)
@@ -328,7 +336,8 @@ def tile_list_meteor_catalogue_scores_kernel(
         load_chunk("w3", w3, 3, "raw_w1")
         load_dealt_gates(0, wg1)
         load_dealt_gates(1, wg2)
-        load_bg(0, 0, "bg_first")
+        load_bg(0, 0, None)
+        load_bg(0, 1, "big0")
         load_bg(1, 0, None)
         load_bg(1, 1, None)
         load_plane_rows(w4_plane[:].bitcast(I32), w4_scales)
@@ -341,12 +350,13 @@ def tile_list_meteor_catalogue_scores_kernel(
         gather(v_plane, tab_plane[:], 0)
         quantise_weight("w1", 0)
         gather(v_words[0][1], table[0][1][:].bitcast(U32), 0)
-        for s in range(2):
-            trail_features(s)
-            place_trails(s)
+        trail_features(0)
+        place_trails(0)
+        quantise_weight("w1", 1)
+        trail_features(1)
+        place_trails(1)
         for a in range(PASSES):
             gather(v2_plane[a], tab2_plane[:, a * T : (a + 1) * T], 1)
-        quantise_weight("w1", 1)
         quantise_weight("w3", 0)
         trail_features(2)
         place_trails(2)
@@ -356,7 +366,7 @@ def tile_list_meteor_catalogue_scores_kernel(
         deal_w2()
         for name, pair in (("w3", 1), ("w1", 2), ("w1", 3), ("w3", 2), ("w3", 3)):
             quantise_weight(name, pair)
-        z_rows.append([kept([P, PACK, HALF], BF16, "z_rows1_0", "tab2_plane"), stage_pool.tile([P, PACK, HALF], BF16, name="z_rows1_1", tag="stage", align_bytes=64)])
+        z_rows.append([kept([P, PACK, HALF], BF16, "z_rows1_0", "tab2_plane"), kept([P, PACK, HALF], BF16, "z_rows1_1", "held")])
         back_banks = {4: [bank_h1[0], bank_back[0]], 5: [bank_h1[1], bank_w2[0]], 6: [bank_h1[0], bank_w2[1]]}
         for s in range(SLICES - 1):
             place_radiants(s)
@@ -368,7 +378,6 @@ def tile_list_meteor_catalogue_scores_kernel(
                 for n, bank in enumerate(bank_back + [bank_h1[1]]):
                     make_z_rows(n % 2, n // 2, bank)
             elif s == 5:
-                load_bg(0, 1, "bg_first")
                 join_pages(s)
                 for n, bank in enumerate([bank_back[1], bank_back[2], bank_back[0], bank_h1[0]]):
                     make_z_rows(n % 2, 2 + n // 2, bank)
@@ -384,11 +393,6 @@ def tile_list_meteor_catalogue_scores_kernel(
         spent_words = ("words_w3_0", "words_w3_1", "words_w1_3", "words_w3_2")
         z_words.append([kept([P, QUARTER], U32, "z_words1_%d" % c, spent_words[c]) for c in range(QUARTERS)])
         out_banks = [bank_back[1], bank_back[2], bank_back[0], bank_h1[1], bank_w2[0], bank_w3, bank_h1[0], bank_w2[1]]
-        for h in range(HALVES):
-            project(0, h)
-        last_z_rows()
         for c in range(QUARTERS):
-            quantise_z(1, c)
-            project(1, c)
-            if c % 2 == 1:
-                store(c // 2)
+            project(0, c)
+        last_z_rows()

@@ -81,14 +81,22 @@ def tile_list_meteor_catalogue_scores_kernel(
         turned = {}
         wg_dealt = []
         dealt = []
-        held = {("w1", 1): kept([P, PASSES, CHUNK, PACK], BF16, "held")}
-        h1_second = held["w1", 1][:].rearrange("p a c j -> p (a c j)")[:, : 2 * S].bitcast(F32)
+        held_tile = kept([P, PASSES, CHUNK, PACK], BF16, "held")
+        held = {("w1", 1): held_tile, ("w1", 2): held_tile}
+        h1_second = held_tile[:].rearrange("p a c j -> p (a c j)")[:, : 2 * S].bitcast(F32)
 
         def clear(tile_ap):
             nc.vector.memset(tile_ap.bitcast(I32), 0)
 
         def load_words(i, words, a):
             nc.sync.dma_start(table[i][a][:], words[a].rearrange("p t i -> p (t i)").bitcast(I32))
+
+        def load_packed_plane(plane, scales):
+            for quad in range(4):
+                nc.sync.dma_start(
+                    plane[32 * quad : 32 * quad + 4 * PASSES, :].bitcast(I32),
+                    scales[:, 4 * quad : 4 * quad + 4, :].bitcast(I32),
+                )
 
         def load_plane_rows(plane, scales):
             for quad in range(4):
@@ -124,6 +132,11 @@ def tile_list_meteor_catalogue_scores_kernel(
                 nc.sync.dma_start(tile[32 * quad : 32 * (quad + 1)], wg.rearrange("(q t) j -> q t j", t=PACK))
             wg_dealt.append(tile)
 
+        def plain_columns(name, pair, a):
+            if (name, pair * CHUNK, a) in raw and raw[name, pair * CHUNK, a].shape[2] == CHUNK:
+                return raw[name, pair * CHUNK, a][:]
+            return raw[name, 0, a][:, :, pair * CHUNK : (pair + 1) * CHUNK]
+
         def quantise_weight(name, pair):
             if (name, pair) in held:
                 grouped = held[name, pair]
@@ -133,7 +146,7 @@ def tile_list_meteor_catalogue_scores_kernel(
                 if pair < 2:
                     nc.scalar.copy(
                         grouped[:, a].rearrange("p (c i) j -> p c j i", i=4),
-                        raw[name, pair * CHUNK, a][:].rearrange("p j (c i) -> p c j i", i=4),
+                        plain_columns(name, pair, a).rearrange("p j (c i) -> p c j i", i=4),
                     )
                     continue
                 for c0 in [c0 for (other, c0, b) in raw if other == name and b == a and c0 >= K_PASS]:
@@ -189,7 +202,7 @@ def tile_list_meteor_catalogue_scores_kernel(
                     v_words[1][a][:].bitcast(FP8X4), v2_plane[a][:], start=a == 0, stop=a == PASSES - 1,
                 )
             product(bank_w3, "w3", s, 1, [v2_plane[a][:] for a in range(PASSES)])
-            nc.scalar.copy(sum2_sb[s % 2][:], bank_w2[s % 2][:])
+            nc.scalar.copy(h1_second if s == 2 else sum2_sb[s % 2][:], bank_w2[s % 2][:])
 
         def gates(i, s):
             return wg_sb[i][:] if s < 4 else wg_dealt[i][:, s - 4, :]
@@ -198,12 +211,13 @@ def tile_list_meteor_catalogue_scores_kernel(
             nc.vector.tensor_tensor(page_a[s % 3][:].indirect(idx[2][:]), h1_second if s == 1 else h1_sb[s % 3][:], gates(0, s), ALU.mult)
 
         def place_radiants(s):
-            spent = {5: (0, 1), 6: (0, 3), 7: (1, 1)}
+            spent = {5: (0, 0), 6: (0, 2), 7: (1, 1)}
+            sum2 = h1_second if s == 2 else sum2_sb[s % 2][:]
             if s in spent:
                 h2 = bg_sb[spent[s]][:, HALF:]
             else:
-                h2 = sum2_sb[s % 2][:]
-            nc.vector.tensor_tensor(h2, bank_w3[:], sum2_sb[s % 2][:], ALU.max)
+                h2 = sum2
+            nc.vector.tensor_tensor(h2, bank_w3[:], sum2, ALU.max)
             nc.vector.tensor_tensor(page_b[s % 2][:].indirect(idx[3][:]), h2, gates(1, s), ALU.mult)
 
         def add_turned(bank, first, second):
@@ -227,7 +241,8 @@ def tile_list_meteor_catalogue_scores_kernel(
                     nc.scalar.activation(turned[0, h][:, :, :, rows], q_t, ACT.Silu, scale=-2.0)
                     nc.scalar.copy(turned[1, h][:, :, :, rows], q_t)
                 return
-            both = [raw_pool.tile([P, T2], F32, name="turned%d_%d" % (s, kind), tag="raw_w3") for kind in range(2)]
+            pair = kept([P, 2, T2], F32, "turned_slice%d" % s, "raw_w3_%d" % (s % 2))
+            both = [pair[:, kind, :] for kind in range(2)]
             for h in range(HALVES):
                 cols = slice(h * HALF, (h + 1) * HALF)
                 nc.scalar.activation(both[0][:, cols], banks[h][:], ACT.Silu, scale=-2.0)
@@ -313,28 +328,23 @@ def tile_list_meteor_catalogue_scores_kernel(
             nc.sync.dma_start(tile[:], offsets)
         nc.sync.dma_start(gain_sb[:], gain.rearrange("(b p t) -> p b t", b=BLOCKS, t=PACK))
         load_words(0, tab_words, 0)
-        for quad in range(4):
-            nc.sync.dma_start(
-                tab_plane[32 * quad : 32 * quad + 4 * PASSES, :].bitcast(I32),
-                tab_scales[:, 4 * quad : 4 * quad + 4, :].bitcast(I32),
-            )
+        load_packed_plane(tab_plane, tab_scales)
         load_chunk("w1", w1, 0, "raw_w1")
         load_words(0, tab_words, 1)
         nc.sync.dma_start(wg_sb[0][:], wg1)
         load_chunk("w1", w1, 1, "raw_w1")
         load_words(1, tab2_words, 0)
         load_plane_rows(tab2_plane[:].bitcast(I32).rearrange("p (a t) -> p a t", a=PASSES), tab2_scales)
-        load_chunk("w3", w3, 0, "raw_w3")
-        load_chunk("w3", w3, 1, "raw_w3")
-        load_weight("w1", w1, K_PASS, K_PASS, [kept([P, PACK, K_PASS], F32, "raw_w1_b%d" % a, "big%d" % a) for a in range(PASSES)])
+        load_weight("w3", w3, 0, K_PASS, [kept([P, PACK, K_PASS], F32, "raw_w3_%d" % a) for a in range(PASSES)])
         load_plane_rows(w2_plane[:].bitcast(I32), w2_scales)
         load_w2(0)
         nc.sync.dma_start(wg_sb[1][:], wg2)
         load_words(1, tab2_words, 1)
         load_w2(1)
+        load_weight("w1", w1, K_PASS, K_PASS, [kept([P, PACK, K_PASS], F32, "raw_w1_b%d" % a, "big%d" % a) for a in range(PASSES)])
+        load_dealt_gates(0, wg1)
         load_chunk("w3", w3, 2, "raw_w1")
         load_chunk("w3", w3, 3, "raw_w1")
-        load_dealt_gates(0, wg1)
         load_dealt_gates(1, wg2)
         load_bg(0, 0, None)
         load_bg(0, 1, "big0")
@@ -364,15 +374,18 @@ def tile_list_meteor_catalogue_scores_kernel(
             gather(v_words[1][a], table[1][a][:].bitcast(U32), 1)
         radiant_sums(0)
         deal_w2()
-        for name, pair in (("w3", 1), ("w1", 2), ("w1", 3), ("w3", 2), ("w3", 3)):
+        for name, pair in (("w3", 1), ("w1", 2)):
             quantise_weight(name, pair)
         z_rows.append([kept([P, PACK, HALF], BF16, "z_rows1_0", "tab2_plane"), kept([P, PACK, HALF], BF16, "z_rows1_1", "held")])
+        late = {0: ("w1", 3), 1: ("w3", 2), 3: ("w3", 3)}
         back_banks = {4: [bank_h1[0], bank_back[0]], 5: [bank_h1[1], bank_w2[0]], 6: [bank_h1[0], bank_w2[1]]}
         for s in range(SLICES - 1):
             place_radiants(s)
             if 1 <= s < SLICES - 2:
                 place_trails(s + 2)
             radiant_sums(s + 1)
+            if s in late:
+                quantise_weight(*late[s])
             if s == 3:
                 join_pages(s)
                 for n, bank in enumerate(bank_back + [bank_h1[1]]):

@@ -22,13 +22,16 @@ PACK = 4
 K_PASS = P * PACK
 PASSES = K // K_PASS
 SLICES = H // P
-BLOCKS = H // K_PASS
+PARTS = H // K_PASS
+PLAIN = SLICES // PARTS
 HALF = 512
 HALVES = T2 // HALF
 QUARTER = 256
 QUARTERS = T2 // QUARTER
 CHUNK = 2 * P
-CHUNKS = H // CHUNK
+PAGES_A, PAGES_B = 3, 2
+W3_LEAD = 2
+STAGES = 4
 
 
 def tile_list_meteor_catalogue_scores_kernel(
@@ -39,8 +42,8 @@ def tile_list_meteor_catalogue_scores_kernel(
     with ExitStack() as ctx:
         lists = ctx.enter_context(tc.tile_pool(name="lists", bufs=1))
         keep = ctx.enter_context(tc.tile_pool(name="keep", bufs=1))
-        raw_pool = ctx.enter_context(tc.tile_pool(name="raw", bufs=4))
-        stage_pool = ctx.enter_context(tc.tile_pool(name="stage", bufs=4))
+        raw_pool = ctx.enter_context(tc.tile_pool(name="raw", bufs=2 * PASSES))
+        stage_pool = ctx.enter_context(tc.tile_pool(name="stage", bufs=STAGES))
         psum = ctx.enter_context(tc.psum_pool(name="psum", bufs=1))
 
         def kept(shape, dtype, name, tag=None):
@@ -49,25 +52,26 @@ def tile_list_meteor_catalogue_scores_kernel(
         idx = [lists.tile([P, S // 16], U16, name="idx%d" % i) for i in range(4)]
         table = [[kept([P, T], I32, "tab%d_%d" % (i, a), "big%d" % (2 * i + a)) for a in range(PASSES)] for i in range(2)]
         tab_plane = kept([P, T], U8, "tab_plane")
-        tab2_plane = kept([P, PASSES * T], U8, "tab2_plane")
+        tab2_plane = kept([P, T], U8, "tab2_plane")
         v_words = [[kept([P, S], U32, "v%d_%d" % (i, a)) for a in range(PASSES)] for i in range(2)]
         v_plane = kept([P, S], U8, "v_plane")
-        v2_plane = [kept([P, S], U8, "v2_plane%d" % a) for a in range(PASSES)]
-        w2_sb = [kept([P, PASSES, 2 * K_PASS], U8, "w2_sb%d" % b) for b in range(BLOCKS)]
+        v2_plane = kept([P, S], U8, "v2_plane")
+        v2_plane_moved = kept([P, S], U8, "v2_plane_moved")
+        w2_sb = [kept([P, PASSES, 2 * K_PASS], U8, "w2_sb%d" % b) for b in range(PARTS)]
         w2_plane = kept([P, PASSES, H], U8, "w2_plane")
-        w4_sb = kept([P, BLOCKS, 2 * N], U8, "w4_sb")
-        w4_plane = kept([P, BLOCKS, N], U8, "w4_plane")
+        w4_sb = kept([P, PARTS, 2 * N], U8, "w4_sb")
+        w4_plane = kept([P, PARTS, N], U8, "w4_plane")
         wg_sb = [kept([P, S], F32, "wg%d" % i) for i in range(2)]
-        gain_sb = kept([P, BLOCKS, PACK], F32, "gain_sb")
-        page_a = [kept([P, T2], F32, "page_a%d" % i) for i in range(3)]
-        page_b = [kept([P, T2], F32, "page_b%d" % i) for i in range(2)]
-        h1_sb = [kept([P, S], F32, "h1_%d" % i) for i in range(3)]
+        gain_sb = kept([P, PARTS, PACK], F32, "gain_sb")
+        page_a = [kept([P, T2], F32, "page_a%d" % i) for i in range(PAGES_A)]
+        page_b = [kept([P, T2], F32, "page_b%d" % i) for i in range(PAGES_B)]
+        h1_sb = [kept([P, S], F32, "h1_%d" % i) for i in range(PAGES_A)]
         sum2_sb = [kept([P, S], F32, "sum2_%d" % i) for i in range(2)]
         w2_dealt_plane = kept([P, PASSES, K_PASS], U8, "w2_dealt_plane")
         widths = [HALF, QUARTER]
         z_rows = [[kept([P, PACK, HALF], BF16, "z_rows0_%d" % h) for h in range(HALVES)]]
         z_words = [[kept([P, HALF], U32, "z_words0_%d" % h) for h in range(HALVES)]]
-        z_plane = [[kept([P, widths[b]], U8, "z_plane%d_%d" % (b, c)) for c in range(T2 // widths[b])] for b in range(BLOCKS)]
+        z_plane = [[kept([P, widths[b]], U8, "z_plane%d_%d" % (b, c)) for c in range(T2 // widths[b])] for b in range(PARTS)]
         ident = kept([P, P], F32, "ident")
 
         bank_h1 = [psum.tile([P, HALF], F32, name="bank_h1_%d" % i) for i in range(2)]
@@ -81,9 +85,15 @@ def tile_list_meteor_catalogue_scores_kernel(
         turned = {}
         wg_dealt = []
         dealt = []
-        held_tile = kept([P, PASSES, CHUNK, PACK], BF16, "held")
-        held = {("w1", 1): held_tile, ("w1", 2): held_tile}
-        h1_second = held_tile[:].rearrange("p a c j -> p (a c j)")[:, : 2 * S].bitcast(F32)
+        held = kept([P, PASSES, CHUNK, PACK], BF16, "held")
+        held_pairs = [("w1", 1), ("w1", 2)]
+        held_f32 = held[:].rearrange("p a c j -> p (a c j)")[:, : 2 * S].bitcast(F32)
+
+        def h1_of(s):
+            return held_f32 if s == 1 else h1_sb[s % PAGES_A][:]
+
+        def sum2_of(s):
+            return held_f32 if s == 2 else sum2_sb[s % 2][:]
 
         def clear(tile_ap):
             nc.vector.memset(tile_ap.bitcast(I32), 0)
@@ -111,15 +121,15 @@ def tile_list_meteor_catalogue_scores_kernel(
                 nc.sync.dma_start(tiles[a][:], rows.rearrange("(p j) c -> p j c", j=PACK))
                 raw[name, c0, a] = tiles[a]
 
-        def load_chunk(name, w, chunk, tag):
-            tiles = [raw_pool.tile([P, PACK, CHUNK], F32, name="raw_%s_%d" % (name, chunk), tag=tag) for a in range(PASSES)]
+        def load_chunk(name, w, chunk):
+            tiles = [raw_pool.tile([P, PACK, CHUNK], F32, name="raw_%s_%d" % (name, chunk), tag="chunk") for a in range(PASSES)]
             load_weight(name, w, chunk * CHUNK, CHUNK, tiles)
 
         def load_w2(b):
             words = w2_words[:, :, 2 * K_PASS * b : 2 * K_PASS * (b + 1)]
             nc.sync.dma_start(w2_sb[b][:].bitcast(I32), words.bitcast(I32).rearrange("a p c -> p a c"))
 
-        def load_bg(b, u, tag):
+        def load_bg(b, u, tag=None):
             rows = bg[b * K_PASS : (b + 1) * K_PASS, :].rearrange("(p t) m -> p t m", t=PACK)
             tile = kept([P, 2, T2], F32, "bg%d_%d" % (b, u), tag)
             nc.sync.dma_start(tile[:], rows[:, 2 * u : 2 * u + 2, :])
@@ -133,28 +143,29 @@ def tile_list_meteor_catalogue_scores_kernel(
             wg_dealt.append(tile)
 
         def plain_columns(name, pair, a):
-            if (name, pair * CHUNK, a) in raw and raw[name, pair * CHUNK, a].shape[2] == CHUNK:
+            if name == "w1":
                 return raw[name, pair * CHUNK, a][:]
             return raw[name, 0, a][:, :, pair * CHUNK : (pair + 1) * CHUNK]
 
         def quantise_weight(name, pair):
-            if (name, pair) in held:
-                grouped = held[name, pair]
+            if (name, pair) in held_pairs:
+                grouped = held
             else:
                 grouped = stage_pool.tile([P, PASSES, CHUNK, PACK], BF16, name="grouped", tag="stage", align_bytes=64)
             for a in range(PASSES):
-                if pair < 2:
+                if 2 * pair < PLAIN:
                     nc.scalar.copy(
                         grouped[:, a].rearrange("p (c i) j -> p c j i", i=4),
                         plain_columns(name, pair, a).rearrange("p j (c i) -> p c j i", i=4),
                     )
                     continue
-                for c0 in [c0 for (other, c0, b) in raw if other == name and b == a and c0 >= K_PASS]:
+                t0 = 2 * pair - PLAIN
+                for c0 in [c0 for (other, c0, step) in raw if other == name and step == a and c0 >= K_PASS]:
                     source = raw[name, c0, a][:].rearrange("p j (q t) -> p q j t", t=PACK)
                     q0 = (c0 - K_PASS) // PACK
                     nc.scalar.copy(
                         grouped[:, a].rearrange("p (e q) j -> p q j e", e=2)[:, q0 : q0 + source.shape[1]],
-                        source[:, :, :, 2 * (pair - 2) : 2 * (pair - 1)],
+                        source[:, :, :, t0 : t0 + 2],
                     )
             words = kept([P, PASSES, CHUNK], U32, "words_%s_%d" % (name, pair))
             plane = kept([P, PASSES, CHUNK], U8, "plane_%s_%d" % (name, pair))
@@ -179,7 +190,7 @@ def tile_list_meteor_catalogue_scores_kernel(
 
         def trail_features(s):
             product(bank_h1[s % 2], "w1", s, 0, [v_plane[4 * a :, :] for a in range(PASSES)])
-            nc.scalar.activation(h1_second if s == 1 else h1_sb[s % 3][:], bank_h1[s % 2][:], ACT.Tanh)
+            nc.scalar.activation(h1_of(s), bank_h1[s % 2][:], ACT.Tanh)
 
         def deal_w2():
             w2_dealt = kept([P, PASSES, 2 * K_PASS], U8, "w2_dealt", "tab_plane")
@@ -194,34 +205,30 @@ def tile_list_meteor_catalogue_scores_kernel(
             )
 
         def radiant_sums(s):
-            words, plane = (w2_sb[0], w2_plane) if s < 4 else (dealt[0], w2_dealt_plane)
-            c0 = P * (s % 4)
+            words, plane = (w2_sb[0], w2_plane) if s < PLAIN else (dealt[0], w2_dealt_plane)
+            c0 = P * (s % PLAIN)
             for a in range(PASSES):
                 nc.tensor.matmul_mx(
                     bank_w2[s % 2][:], words[:, a, 2 * c0 : 2 * (c0 + P)].bitcast(FP4X4), plane[:, a, c0 : c0 + P],
-                    v_words[1][a][:].bitcast(FP8X4), v2_plane[a][:], start=a == 0, stop=a == PASSES - 1,
+                    v_words[1][a][:].bitcast(FP8X4), (v2_plane, v2_plane_moved)[a][:], start=a == 0, stop=a == PASSES - 1,
                 )
-            product(bank_w3, "w3", s, 1, [v2_plane[a][:] for a in range(PASSES)])
-            nc.scalar.copy(h1_second if s == 2 else sum2_sb[s % 2][:], bank_w2[s % 2][:])
+            product(bank_w3, "w3", s, 1, [v2_plane[4 * a :, :] for a in range(PASSES)])
+            nc.scalar.copy(sum2_of(s), bank_w2[s % 2][:])
 
         def gates(i, s):
-            return wg_sb[i][:] if s < 4 else wg_dealt[i][:, s - 4, :]
+            return wg_sb[i][:] if s < PLAIN else wg_dealt[i][:, s - PLAIN, :]
 
         def place_trails(s):
-            nc.vector.tensor_tensor(page_a[s % 3][:].indirect(idx[2][:]), h1_second if s == 1 else h1_sb[s % 3][:], gates(0, s), ALU.mult)
+            nc.vector.tensor_tensor(page_a[s % PAGES_A][:].indirect(idx[2][:]), h1_of(s), gates(0, s), ALU.mult)
 
         def place_radiants(s):
-            spent = {5: (0, 0), 6: (0, 2), 7: (1, 1)}
-            sum2 = h1_second if s == 2 else sum2_sb[s % 2][:]
-            if s in spent:
-                h2 = bg_sb[spent[s]][:, HALF:]
-            else:
-                h2 = sum2
-            nc.vector.tensor_tensor(h2, bank_w3[:], sum2, ALU.max)
-            nc.vector.tensor_tensor(page_b[s % 2][:].indirect(idx[3][:]), h2, gates(1, s), ALU.mult)
+            spent_bg = {5: (0, 0), 6: (0, 2), 7: (1, 1)}
+            h2 = bg_sb[spent_bg[s]][:, HALF:] if s in spent_bg else sum2_of(s)
+            nc.vector.tensor_tensor(h2, bank_w3[:], sum2_of(s), ALU.max)
+            nc.vector.tensor_tensor(page_b[s % PAGES_B][:].indirect(idx[3][:]), h2, gates(1, s), ALU.mult)
 
         def add_turned(bank, first, second):
-            for g in range(4):
+            for g in range(HALF // P):
                 cols = bank[:, g * P : (g + 1) * P]
                 nc.tensor.matmul(cols, first(g), ident[:], start=True, stop=False, is_transpose=True)
                 nc.tensor.matmul(cols, second(g), ident[:], start=False, stop=True, is_transpose=True)
@@ -231,12 +238,12 @@ def tile_list_meteor_catalogue_scores_kernel(
             for h in range(HALVES):
                 add_turned(
                     banks[h],
-                    lambda g: page_a[s % 3][:, h * HALF + g * P : h * HALF + (g + 1) * P],
-                    lambda g: page_b[s % 2][:, h * HALF + g * P : h * HALF + (g + 1) * P],
+                    lambda g: page_a[s % PAGES_A][:, h * HALF + g * P : h * HALF + (g + 1) * P],
+                    lambda g: page_b[s % PAGES_B][:, h * HALF + g * P : h * HALF + (g + 1) * P],
                 )
-            if s < 4:
+            if s < PLAIN:
                 for h in range(HALVES):
-                    q_t = banks[h][:].rearrange("m (g p t) -> m g t p", g=4, t=PACK)
+                    q_t = banks[h][:].rearrange("m (g p t) -> m g t p", g=HALF // P, t=PACK)
                     rows = slice(32 * s, 32 * (s + 1))
                     nc.scalar.activation(turned[0, h][:, :, :, rows], q_t, ACT.Silu, scale=-2.0)
                     nc.scalar.copy(turned[1, h][:, :, :, rows], q_t)
@@ -258,7 +265,7 @@ def tile_list_meteor_catalogue_scores_kernel(
                     lambda g: both[0][:, h * HALF + g * P : h * HALF + (g + 1) * P],
                     lambda g: both[1][:, h * HALF + g * P : h * HALF + (g + 1) * P],
                 )
-                finish_z(1, h, s - 4, bank[:], bg_sb[1, s - 4][:, h * HALF : (h + 1) * HALF])
+                finish_z(1, h, s - PLAIN, bank[:], bg_sb[1, s - PLAIN][:, h * HALF : (h + 1) * HALF])
 
         def finish_z(b, h, t, values, addend):
             nc.vector.scalar_tensor_tensor(z_rows[b][h][:, t, :], values, gain_sb[:, b, t : t + 1], addend, ALU.mult, ALU.add)
@@ -271,7 +278,7 @@ def tile_list_meteor_catalogue_scores_kernel(
             s, t = SLICES - 1, PACK - 1
             q, part, curve = [kept([P, T2], F32, "last%d" % kind, ("turned0_0", "turned1_0", "big1")[kind]) for kind in range(3)]
             for cols in (slice(0, QUARTER), slice(QUARTER, T2)):
-                nc.vector.tensor_tensor(q[:, cols], page_a[s % 3][:, cols], page_b[s % 2][:, cols], ALU.add)
+                nc.vector.tensor_tensor(q[:, cols], page_a[s % PAGES_A][:, cols], page_b[s % PAGES_B][:, cols], ALU.add)
                 nc.scalar.activation(curve[:, cols], q[:, cols], ACT.Silu, scale=-2.0)
             for c in range(QUARTERS):
                 cols = slice(c * QUARTER, (c + 1) * QUARTER)
@@ -287,7 +294,7 @@ def tile_list_meteor_catalogue_scores_kernel(
         def quantise_z(b, c):
             h, m0 = divmod(c * widths[b], HALF)
             grouped = stage_pool.tile([P, widths[b], PACK], BF16, name="z_grouped", tag="stage", align_bytes=64)
-            move = nc.vector.tensor_copy if b == 1 and c % 2 == 1 else nc.scalar.copy
+            move = nc.vector.tensor_copy if b == 1 else nc.scalar.copy
             move(
                 grouped[:].rearrange("p (c i) t -> p c t i", i=4),
                 z_rows[b][h][:, :, m0 : m0 + widths[b]].rearrange("p t (c i) -> p c t i", i=4),
@@ -311,8 +318,7 @@ def tile_list_meteor_catalogue_scores_kernel(
             spent_tiles = ("sum2_0", "sum2_1", "h1_0", "h1_1", "h1_2", "words_w1_0", "words_w1_1", "words_w1_2")
             for pair in range(2):
                 res = kept([P, 2, QUARTER], F32, "res%d_%d" % (c, pair), spent_tiles[2 * c + pair])
-                move = nc.vector.tensor_copy if c == 3 and pair == 0 else nc.scalar.copy
-                move(res[:].rearrange("p e m -> p (e m)"), out_banks[2 * c + pair][:])
+                nc.scalar.copy(res[:].rearrange("p e m -> p (e m)"), out_banks[2 * c + pair][:])
                 rows = out[2 * pair * P : 2 * (pair + 1) * P, c * QUARTER : (c + 1) * QUARTER]
                 nc.sync.dma_start(rows.rearrange("(e p) m -> p e m", e=2), res[:])
 
@@ -320,42 +326,45 @@ def tile_list_meteor_catalogue_scores_kernel(
         clear(tab2_plane[:])
         clear(page_a[0][:])
         clear(page_a[1][:])
-        for tile in (w2_plane, page_a[2], page_b[0], page_b[1], w4_plane):
+        for tile in (w2_plane, v2_plane_moved, page_a[2], page_b[0], page_b[1], w4_plane):
             nc.gpsimd.memset(tile[:].bitcast(I32), 0)
         make_identity(nc, ident[:])
 
         for tile, offsets in zip(idx, (offs, offs2, offs3, offs4)):
             nc.sync.dma_start(tile[:], offsets)
-        nc.sync.dma_start(gain_sb[:], gain.rearrange("(b p t) -> p b t", b=BLOCKS, t=PACK))
+        nc.sync.dma_start(gain_sb[:], gain.rearrange("(b p t) -> p b t", b=PARTS, t=PACK))
         load_words(0, tab_words, 0)
         load_packed_plane(tab_plane, tab_scales)
-        load_chunk("w1", w1, 0, "raw_w1")
+        load_chunk("w1", w1, 0)
         load_words(0, tab_words, 1)
+        load_packed_plane(tab2_plane, tab2_scales)
         nc.sync.dma_start(wg_sb[0][:], wg1)
-        load_chunk("w1", w1, 1, "raw_w1")
+        load_chunk("w1", w1, 1)
         load_words(1, tab2_words, 0)
-        load_plane_rows(tab2_plane[:].bitcast(I32).rearrange("p (a t) -> p a t", a=PASSES), tab2_scales)
         load_weight("w3", w3, 0, K_PASS, [kept([P, PACK, K_PASS], F32, "raw_w3_%d" % a) for a in range(PASSES)])
         load_plane_rows(w2_plane[:].bitcast(I32), w2_scales)
         load_w2(0)
+        gather(v2_plane, tab2_plane[:], 1)
+        nc.sync.dma_start(v2_plane_moved[: P - 4].bitcast(I32), v2_plane[4:].bitcast(I32))
         nc.sync.dma_start(wg_sb[1][:], wg2)
         load_words(1, tab2_words, 1)
         load_w2(1)
         load_weight("w1", w1, K_PASS, K_PASS, [kept([P, PACK, K_PASS], F32, "raw_w1_b%d" % a, "big%d" % a) for a in range(PASSES)])
         load_dealt_gates(0, wg1)
-        load_chunk("w3", w3, 2, "raw_w1")
-        load_chunk("w3", w3, 3, "raw_w1")
+        load_chunk("w3", w3, 2)
+        load_chunk("w3", w3, 3)
         load_dealt_gates(1, wg2)
-        load_bg(0, 0, None)
+        load_bg(0, 0)
         load_bg(0, 1, "big0")
-        load_bg(1, 0, None)
-        load_bg(1, 1, None)
+        load_bg(1, 0)
+        load_bg(1, 1)
         load_plane_rows(w4_plane[:].bitcast(I32), w4_scales)
         nc.sync.dma_start(w4_sb[:].bitcast(I32), w4_words.bitcast(I32).rearrange("a p c -> p a c"))
 
         for kind in range(2):
             for h in range(HALVES):
-                turned[kind, h] = kept([P, 4, PACK, P], F32, "turned%d_%d" % (kind, h))
+                turned[kind, h] = kept([P, HALF // P, PACK, P], F32, "turned%d_%d" % (kind, h))
+
         gather(v_words[0][0], table[0][0][:].bitcast(U32), 0)
         gather(v_plane, tab_plane[:], 0)
         quantise_weight("w1", 0)
@@ -365,8 +374,6 @@ def tile_list_meteor_catalogue_scores_kernel(
         quantise_weight("w1", 1)
         trail_features(1)
         place_trails(1)
-        for a in range(PASSES):
-            gather(v2_plane[a], tab2_plane[:, a * T : (a + 1) * T], 1)
         quantise_weight("w3", 0)
         trail_features(2)
         place_trails(2)
@@ -377,7 +384,7 @@ def tile_list_meteor_catalogue_scores_kernel(
         for name, pair in (("w3", 1), ("w1", 2)):
             quantise_weight(name, pair)
         z_rows.append([kept([P, PACK, HALF], BF16, "z_rows1_0", "tab2_plane"), kept([P, PACK, HALF], BF16, "z_rows1_1", "held")])
-        late = {0: ("w1", 3), 1: ("w3", 2), 3: ("w3", 3)}
+        late = {0: ("w1", 3), **{2 * pair - 1 - W3_LEAD: ("w3", pair) for pair in (2, 3)}}
         back_banks = {4: [bank_h1[0], bank_back[0]], 5: [bank_h1[1], bank_w2[0]], 6: [bank_h1[0], bank_w2[1]]}
         for s in range(SLICES - 1):
             place_radiants(s)
@@ -386,19 +393,16 @@ def tile_list_meteor_catalogue_scores_kernel(
             radiant_sums(s + 1)
             if s in late:
                 quantise_weight(*late[s])
-            if s == 3:
-                join_pages(s)
+            join_pages(s)
+            if s == PLAIN - 1:
                 for n, bank in enumerate(bank_back + [bank_h1[1]]):
                     make_z_rows(n % 2, n // 2, bank)
-            elif s == 5:
-                join_pages(s)
+            if s == PLAIN + 1:
                 for n, bank in enumerate([bank_back[1], bank_back[2], bank_back[0], bank_h1[0]]):
                     make_z_rows(n % 2, 2 + n // 2, bank)
                 for h in range(HALVES):
                     quantise_z(0, h)
-            else:
-                join_pages(s)
-            if s >= 4:
+            if s >= PLAIN:
                 turn_back(s)
             if s + 3 < SLICES:
                 trail_features(s + 3)

from contextlib import ExitStack

import concourse.mybir as mybir
from concourse.masks import make_identity

K, T, S, H, N, T2 = 1024, 2048, 512, 1024, 512, 1024
FLOPS = 2 * (3 * K * H * S + H * N * T2)

F32 = mybir.dt.float32
BF16 = mybir.dt.bfloat16
I32 = mybir.dt.int32
U32 = mybir.dt.uint32
U16 = mybir.dt.uint16
U8 = mybir.dt.uint8
FP8X4 = mybir.dt.float8_e4m3fn_x4
FP4X4 = mybir.dt.float4_e2m1fn_x4
ACT = mybir.ActivationFunctionType
ALU = mybir.AluOpType

P = 128
PACK = 4
K_PASS = P * PACK
PASSES = K // K_PASS
SLICES = H // P
PARTS = H // K_PASS
PLAIN = SLICES // PARTS
HALF = 512
HALVES = T2 // HALF
QUARTER = 256
QUARTERS = T2 // QUARTER
CHUNK = 2 * P
PAGES_A, PAGES_B = 3, 2
W3_LEAD = 2
STAGES = 4


def tile_list_meteor_catalogue_scores_kernel(
    tc, tab_words, tab_scales, tab2_words, tab2_scales, w1, w2_words, w2_scales, w3, gain, bg, wg1, wg2,
    w4_words, w4_scales, offs, offs2, offs3, offs4, out,
):
    nc = tc.nc
    with ExitStack() as ctx:
        lists = ctx.enter_context(tc.tile_pool(name="lists", bufs=1))
        keep = ctx.enter_context(tc.tile_pool(name="keep", bufs=1))
        raw_pool = ctx.enter_context(tc.tile_pool(name="raw", bufs=2 * PASSES))
        stage_pool = ctx.enter_context(tc.tile_pool(name="stage", bufs=STAGES))
        psum = ctx.enter_context(tc.psum_pool(name="psum", bufs=1))

        def kept(shape, dtype, name, tag=None):
            return keep.tile(shape, dtype, name=name, tag=tag or name, align_bytes=64)

        idx = [lists.tile([P, S // 16], U16, name="idx%d" % i) for i in range(4)]
        table = [[kept([P, T], I32, "tab%d_%d" % (i, a), "big%d" % (2 * i + a)) for a in range(PASSES)] for i in range(2)]
        tab_plane = kept([P, T], U8, "tab_plane")
        tab2_plane = kept([P, T], U8, "tab2_plane")
        v_words = [[kept([P, S], U32, "v%d_%d" % (i, a)) for a in range(PASSES)] for i in range(2)]
        v_plane = kept([P, S], U8, "v_plane")
        v2_plane = kept([P, S], U8, "v2_plane")
        v2_plane_moved = kept([P, S], U8, "v2_plane_moved")
        w2_sb = [kept([P, PASSES, 2 * K_PASS], U8, "w2_sb%d" % b) for b in range(PARTS)]
        w2_plane = kept([P, PASSES, H], U8, "w2_plane")
        w4_sb = kept([P, PARTS, 2 * N], U8, "w4_sb")
        w4_plane = kept([P, PARTS, N], U8, "w4_plane")
        wg_sb = [kept([P, S], F32, "wg%d" % i) for i in range(2)]
        gain_sb = kept([P, PARTS, PACK], F32, "gain_sb")
        page_a = [kept([P, T2], F32, "page_a%d" % i) for i in range(PAGES_A)]
        page_b = [kept([P, T2], F32, "page_b%d" % i) for i in range(PAGES_B)]
        h1_sb = [kept([P, S], F32, "h1_%d" % i) for i in range(PAGES_A)]
        sum2_sb = [kept([P, S], F32, "sum2_%d" % i) for i in range(2)]
        w2_dealt_plane = kept([P, PASSES, K_PASS], U8, "w2_dealt_plane")
        widths = [HALF, QUARTER]
        z_rows = [[kept([P, PACK, HALF], BF16, "z_rows0_%d" % h) for h in range(HALVES)]]
        z_words = [[kept([P, HALF], U32, "z_words0_%d" % h) for h in range(HALVES)]]
        z_plane = [[kept([P, widths[b]], U8, "z_plane%d_%d" % (b, c)) for c in range(T2 // widths[b])] for b in range(PARTS)]
        ident = kept([P, P], F32, "ident")

        bank_h1 = [psum.tile([P, HALF], F32, name="bank_h1_%d" % i) for i in range(2)]
        bank_w2 = [psum.tile([P, HALF], F32, name="bank_w2_%d" % i) for i in range(2)]
        bank_w3 = psum.tile([P, HALF], F32, name="bank_w3")
        bank_back = [psum.tile([P, HALF], F32, name="bank_back%d" % i) for i in range(3)]

        raw = {}
        codes = {}
        bg_sb = {}
        turned = {}
        wg_dealt = []
        dealt = []
        held = kept([P, PASSES, CHUNK, PACK], BF16, "held")
        held_pairs = [("w1", 1), ("w1", 2)]
        held_f32 = held[:].rearrange("p a c j -> p (a c j)")[:, : 2 * S].bitcast(F32)

        def h1_of(s):
            return held_f32 if s == 1 else h1_sb[s % PAGES_A][:]

        def sum2_of(s):
            return held_f32 if s == 2 else sum2_sb[s % 2][:]

        def clear(tile_ap):
            nc.vector.memset(tile_ap.bitcast(I32), 0)

        def load_words(i, words, a):
            nc.sync.dma_start(table[i][a][:], words[a].rearrange("p t i -> p (t i)").bitcast(I32))

        def load_packed_plane(plane, scales):
            for quad in range(4):
                nc.sync.dma_start(
                    plane[32 * quad : 32 * quad + 4 * PASSES, :].bitcast(I32),
                    scales[:, 4 * quad : 4 * quad + 4, :].bitcast(I32),
                )

        def load_plane_rows(plane, scales):
            for quad in range(4):
                nc.sync.dma_start(
                    plane[32 * quad : 32 * quad + 4],
                    scales[:, 4 * quad : 4 * quad + 4, :].bitcast(I32).rearrange("a r c -> r a c"),
                )

        def load_weight(name, w, c0, width, tiles):
            for a in range(PASSES):
                rows = w[a * K_PASS : (a + 1) * K_PASS, c0 : c0 + width]
                nc.sync.dma_start(tiles[a][:], rows.rearrange("(p j) c -> p j c", j=PACK))
                raw[name, c0, a] = tiles[a]

        def load_chunk(name, w, chunk):
            tiles = [raw_pool.tile([P, PACK, CHUNK], F32, name="raw_%s_%d" % (name, chunk), tag="chunk") for a in range(PASSES)]
            load_weight(name, w, chunk * CHUNK, CHUNK, tiles)

        def load_w2(b):
            words = w2_words[:, :, 2 * K_PASS * b : 2 * K_PASS * (b + 1)]
            nc.sync.dma_start(w2_sb[b][:].bitcast(I32), words.bitcast(I32).rearrange("a p c -> p a c"))

        def load_bg(b, u, tag=None):
            rows = bg[b * K_PASS : (b + 1) * K_PASS, :].rearrange("(p t) m -> p t m", t=PACK)
            tile = kept([P, 2, T2], F32, "bg%d_%d" % (b, u), tag)
            nc.sync.dma_start(tile[:], rows[:, 2 * u : 2 * u + 2, :])
            for e in range(2):
                bg_sb[b, 2 * u + e] = tile[:, e, :]

        def load_dealt_gates(i, wg):
            tile = kept([P, PACK, S], F32, "wg_dealt%d" % i, "big%d" % (2 + i))
            for quad in range(4):
                nc.sync.dma_start(tile[32 * quad : 32 * (quad + 1)], wg.rearrange("(q t) j -> q t j", t=PACK))
            wg_dealt.append(tile)

        def plain_columns(name, pair, a):
            if name == "w1":
                return raw[name, pair * CHUNK, a][:]
            return raw[name, 0, a][:, :, pair * CHUNK : (pair + 1) * CHUNK]

        def quantise_weight(name, pair):
            if (name, pair) in held_pairs:
                grouped = held
            else:
                grouped = stage_pool.tile([P, PASSES, CHUNK, PACK], BF16, name="grouped", tag="stage", align_bytes=64)
            for a in range(PASSES):
                if 2 * pair < PLAIN:
                    nc.scalar.copy(
                        grouped[:, a].rearrange("p (c i) j -> p c j i", i=4),
                        plain_columns(name, pair, a).rearrange("p j (c i) -> p c j i", i=4),
                    )
                    continue
                t0 = 2 * pair - PLAIN
                for c0 in [c0 for (other, c0, step) in raw if other == name and step == a and c0 >= K_PASS]:
                    source = raw[name, c0, a][:].rearrange("p j (q t) -> p q j t", t=PACK)
                    q0 = (c0 - K_PASS) // PACK
                    nc.scalar.copy(
                        grouped[:, a].rearrange("p (e q) j -> p q j e", e=2)[:, q0 : q0 + source.shape[1]],
                        source[:, :, :, t0 : t0 + 2],
                    )
            words = kept([P, PASSES, CHUNK], U32, "words_%s_%d" % (name, pair))
            plane = kept([P, PASSES, CHUNK], U8, "plane_%s_%d" % (name, pair))
            nc.vector.quantize_mx(
                words[:].rearrange("p a c -> p (a c)").bitcast(FP8X4),
                plane[:].rearrange("p a c -> p (a c)"),
                grouped[:].rearrange("p a c j -> p (a c j)"),
            )
            for e in range(2):
                codes[name, 2 * pair + e] = (words, plane, e * P)

        def gather(dst, window, i):
            nc.vector.tensor_copy(dst[:], window.indirect(idx[i][:]))

        def product(bank, name, s, i, planes):
            words, plane, c0 = codes[name, s]
            for a in range(PASSES):
                nc.tensor.matmul_mx(
                    bank[:], words[:, a, c0 : c0 + P].bitcast(FP8X4), plane[:, a, c0 : c0 + P],
                    v_words[i][a][:].bitcast(FP8X4), planes[a], start=a == 0, stop=a == PASSES - 1,
                )

        def trail_features(s):
            product(bank_h1[s % 2], "w1", s, 0, [v_plane[4 * a :, :] for a in range(PASSES)])
            nc.scalar.activation(h1_of(s), bank_h1[s % 2][:], ACT.Tanh)

        def deal_w2():
            w2_dealt = kept([P, PASSES, 2 * K_PASS], U8, "w2_dealt", "tab_plane")
            dealt.append(w2_dealt)
            nc.vector.tensor_copy(
                w2_dealt[:].bitcast(U16).rearrange("p a (t q) -> p a t q", t=PACK),
                w2_sb[1][:].bitcast(U16).rearrange("p a (q t) -> p a t q", t=PACK),
            )
            nc.vector.tensor_copy(
                w2_dealt_plane[:].rearrange("p a (t q) -> p a t q", t=PACK),
                w2_plane[:, :, K_PASS:].rearrange("p a (q t) -> p a t q", t=PACK),
            )

        def radiant_sums(s):
            words, plane = (w2_sb[0], w2_plane) if s < PLAIN else (dealt[0], w2_dealt_plane)
            c0 = P * (s % PLAIN)
            for a in range(PASSES):
                nc.tensor.matmul_mx(
                    bank_w2[s % 2][:], words[:, a, 2 * c0 : 2 * (c0 + P)].bitcast(FP4X4), plane[:, a, c0 : c0 + P],
                    v_words[1][a][:].bitcast(FP8X4), (v2_plane, v2_plane_moved)[a][:], start=a == 0, stop=a == PASSES - 1,
                )
            product(bank_w3, "w3", s, 1, [v2_plane[4 * a :, :] for a in range(PASSES)])
            nc.scalar.copy(sum2_of(s), bank_w2[s % 2][:])

        def gates(i, s):
            return wg_sb[i][:] if s < PLAIN else wg_dealt[i][:, s - PLAIN, :]

        def place_trails(s):
            nc.vector.tensor_tensor(page_a[s % PAGES_A][:].indirect(idx[2][:]), h1_of(s), gates(0, s), ALU.mult)

        def place_radiants(s):
            spent_bg = {5: (0, 0), 6: (0, 2), 7: (1, 1)}
            h2 = bg_sb[spent_bg[s]][:, HALF:] if s in spent_bg else sum2_of(s)
            nc.vector.tensor_tensor(h2, bank_w3[:], sum2_of(s), ALU.max)
            nc.vector.tensor_tensor(page_b[s % PAGES_B][:].indirect(idx[3][:]), h2, gates(1, s), ALU.mult)

        def add_turned(bank, first, second):
            for g in range(HALF // P):
                cols = bank[:, g * P : (g + 1) * P]
                nc.tensor.matmul(cols, first(g), ident[:], start=True, stop=False, is_transpose=True)
                nc.tensor.matmul(cols, second(g), ident[:], start=False, stop=True, is_transpose=True)

        def join_pages(s):
            banks = [bank_h1[s % 2], bank_w2[(s + 1) % 2]]
            for h in range(HALVES):
                add_turned(
                    banks[h],
                    lambda g: page_a[s % PAGES_A][:, h * HALF + g * P : h * HALF + (g + 1) * P],
                    lambda g: page_b[s % PAGES_B][:, h * HALF + g * P : h * HALF + (g + 1) * P],
                )
            if s < PLAIN:
                for h in range(HALVES):
                    q_t = banks[h][:].rearrange("m (g p t) -> m g t p", g=HALF // P, t=PACK)
                    rows = slice(32 * s, 32 * (s + 1))
                    nc.scalar.activation(turned[0, h][:, :, :, rows], q_t, ACT.Silu, scale=-2.0)
                    nc.scalar.copy(turned[1, h][:, :, :, rows], q_t)
                return
            pair = kept([P, 2, T2], F32, "turned_slice%d" % s, "raw_w3_%d" % (s % 2))
            both = [pair[:, kind, :] for kind in range(2)]
            for h in range(HALVES):
                cols = slice(h * HALF, (h + 1) * HALF)
                nc.scalar.activation(both[0][:, cols], banks[h][:], ACT.Silu, scale=-2.0)
                nc.scalar.copy(both[1][:, cols], banks[h][:])
            turned[s] = both

        def turn_back(s):
            both = turned[s]
            for h in range(HALVES):
                bank = back_banks[s][h]
                add_turned(
                    bank,
                    lambda g: both[0][:, h * HALF + g * P : h * HALF + (g + 1) * P],
                    lambda g: both[1][:, h * HALF + g * P : h * HALF + (g + 1) * P],
                )
                finish_z(1, h, s - PLAIN, bank[:], bg_sb[1, s - PLAIN][:, h * HALF : (h + 1) * HALF])

        def finish_z(b, h, t, values, addend):
            nc.vector.scalar_tensor_tensor(z_rows[b][h][:, t, :], values, gain_sb[:, b, t : t + 1], addend, ALU.mult, ALU.add)

        def make_z_rows(h, t, bank):
            add_turned(bank, lambda g: turned[0, h][:, g, t, :], lambda g: turned[1, h][:, g, t, :])
            finish_z(0, h, t, bank[:], bg_sb[0, t][:, h * HALF : (h + 1) * HALF])

        def last_z_rows():
            s, t = SLICES - 1, PACK - 1
            q, part, curve = [kept([P, T2], F32, "last%d" % kind, ("turned0_0", "turned1_0", "big1")[kind]) for kind in range(3)]
            for cols in (slice(0, QUARTER), slice(QUARTER, T2)):
                nc.vector.tensor_tensor(q[:, cols], page_a[s % PAGES_A][:, cols], page_b[s % PAGES_B][:, cols], ALU.add)
                nc.scalar.activation(curve[:, cols], q[:, cols], ACT.Silu, scale=-2.0)
            for c in range(QUARTERS):
                cols = slice(c * QUARTER, (c + 1) * QUARTER)
                h, m0 = divmod(c * QUARTER, HALF)
                nc.vector.scalar_tensor_tensor(part[:, cols], q[:, cols], gain_sb[:, 1, t : t + 1], bg_sb[1, t][:, cols], ALU.mult, ALU.add)
                nc.vector.scalar_tensor_tensor(
                    z_rows[1][h][:, t, m0 : m0 + QUARTER], curve[:, cols], gain_sb[:, 1, t : t + 1], part[:, cols], ALU.mult, ALU.add
                )
                quantise_z(1, c)
                project(1, c)
                store(c)

        def quantise_z(b, c):
            h, m0 = divmod(c * widths[b], HALF)
            grouped = stage_pool.tile([P, widths[b], PACK], BF16, name="z_grouped", tag="stage", align_bytes=64)
            move = nc.vector.tensor_copy if b == 1 else nc.scalar.copy
            move(
                grouped[:].rearrange("p (c i) t -> p c t i", i=4),
                z_rows[b][h][:, :, m0 : m0 + widths[b]].rearrange("p t (c i) -> p c t i", i=4),
            )
            nc.vector.quantize_mx(
                z_words[b][c][:].bitcast(FP8X4), z_plane[b][c][:], grouped[:].rearrange("p m t -> p (m t)")
            )

        def project(b, c):
            piece, m0 = divmod(c * QUARTER, widths[b])
            for nt in range(N // P):
                pair, e = divmod(nt, 2)
                nc.tensor.matmul_mx(
                    out_banks[2 * c + pair][:, e * QUARTER : (e + 1) * QUARTER],
                    w4_sb[:, b, 2 * P * nt : 2 * P * (nt + 1)].bitcast(FP4X4), w4_plane[:, b, P * nt : P * (nt + 1)],
                    z_words[b][piece][:, m0 : m0 + QUARTER].bitcast(FP8X4), z_plane[b][piece][:, m0 : m0 + QUARTER],
                    start=b == 0 and e == 0, stop=b == 1 and e == 1,
                )

        def store(c):
            spent_tiles = ("sum2_0", "sum2_1", "h1_0", "h1_1", "h1_2", "words_w1_0", "words_w1_1", "words_w1_2")
            for pair in range(2):
                res = kept([P, 2, QUARTER], F32, "res%d_%d" % (c, pair), spent_tiles[2 * c + pair])
                nc.scalar.copy(res[:].rearrange("p e m -> p (e m)"), out_banks[2 * c + pair][:])
                rows = out[2 * pair * P : 2 * (pair + 1) * P, c * QUARTER : (c + 1) * QUARTER]
                nc.sync.dma_start(rows.rearrange("(e p) m -> p e m", e=2), res[:])

        clear(tab_plane[:])
        clear(tab2_plane[:])
        clear(page_a[0][:])
        clear(page_a[1][:])
        for tile in (w2_plane, v2_plane_moved, page_a[2], page_b[0], page_b[1], w4_plane):
            nc.gpsimd.memset(tile[:].bitcast(I32), 0)
        make_identity(nc, ident[:])

        for tile, offsets in zip(idx, (offs, offs2, offs3, offs4)):
            nc.sync.dma_start(tile[:], offsets)
        nc.sync.dma_start(gain_sb[:], gain.rearrange("(b p t) -> p b t", b=PARTS, t=PACK))
        load_words(0, tab_words, 0)
        load_packed_plane(tab_plane, tab_scales)
        load_chunk("w1", w1, 0)
        load_words(0, tab_words, 1)
        load_packed_plane(tab2_plane, tab2_scales)
        nc.sync.dma_start(wg_sb[0][:], wg1)
        load_chunk("w1", w1, 1)
        load_words(1, tab2_words, 0)
        load_weight("w3", w3, 0, K_PASS, [kept([P, PACK, K_PASS], F32, "raw_w3_%d" % a) for a in range(PASSES)])
        load_plane_rows(w2_plane[:].bitcast(I32), w2_scales)
        load_w2(0)
        gather(v2_plane, tab2_plane[:], 1)
        nc.sync.dma_start(v2_plane_moved[: P - 4].bitcast(I32), v2_plane[4:].bitcast(I32))
        nc.sync.dma_start(wg_sb[1][:], wg2)
        load_words(1, tab2_words, 1)
        load_w2(1)
        load_weight("w1", w1, K_PASS, K_PASS, [kept([P, PACK, K_PASS], F32, "raw_w1_b%d" % a, "big%d" % a) for a in range(PASSES)])
        load_dealt_gates(0, wg1)
        load_chunk("w3", w3, 2)
        load_chunk("w3", w3, 3)
        load_dealt_gates(1, wg2)
        load_bg(0, 0)
        load_bg(0, 1, "big0")
        load_bg(1, 0)
        load_bg(1, 1)
        load_plane_rows(w4_plane[:].bitcast(I32), w4_scales)
        nc.sync.dma_start(w4_sb[:].bitcast(I32), w4_words.bitcast(I32).rearrange("a p c -> p a c"))

        for kind in range(2):
            for h in range(HALVES):
                turned[kind, h] = kept([P, HALF // P, PACK, P], F32, "turned%d_%d" % (kind, h))

        gather(v_words[0][0], table[0][0][:].bitcast(U32), 0)
        gather(v_plane, tab_plane[:], 0)
        quantise_weight("w1", 0)
        gather(v_words[0][1], table[0][1][:].bitcast(U32), 0)
        trail_features(0)
        place_trails(0)
        quantise_weight("w1", 1)
        trail_features(1)
        place_trails(1)
        quantise_weight("w3", 0)
        trail_features(2)
        place_trails(2)
        for a in range(PASSES):
            gather(v_words[1][a], table[1][a][:].bitcast(U32), 1)
        radiant_sums(0)
        deal_w2()
        for name, pair in (("w3", 1), ("w1", 2)):
            quantise_weight(name, pair)
        z_rows.append([kept([P, PACK, HALF], BF16, "z_rows1_0", "tab2_plane"), kept([P, PACK, HALF], BF16, "z_rows1_1", "held")])
        late = {0: ("w1", 3), **{2 * pair - 1 - W3_LEAD: ("w3", pair) for pair in (2, 3)}}
        back_banks = {4: [bank_h1[0], bank_back[0]], 5: [bank_h1[1], bank_w2[0]], 6: [bank_h1[0], bank_w2[1]]}
        for s in range(SLICES - 1):
            place_radiants(s)
            if 1 <= s < SLICES - 2:
                place_trails(s + 2)
            radiant_sums(s + 1)
            if s in late:
                quantise_weight(*late[s])
            join_pages(s)
            if s == PLAIN - 1:
                for n, bank in enumerate(bank_back + [bank_h1[1]]):
                    make_z_rows(n % 2, n // 2, bank)
            if s == PLAIN + 1:
                for n, bank in enumerate([bank_back[1], bank_back[2], bank_back[0], bank_h1[0]]):
                    make_z_rows(n % 2, 2 + n // 2, bank)
                for h in range(HALVES):
                    quantise_z(0, h)
            if s >= PLAIN:
                turn_back(s)
            if s + 3 < SLICES:
                trail_features(s + 3)
        place_radiants(SLICES - 1)
        spent_words = ("words_w3_0", "words_w3_1", "words_w1_3", "words_w3_2")
        z_words.append([kept([P, QUARTER], U32, "z_words1_%d" % c, spent_words[c]) for c in range(QUARTERS)])
        out_banks = [bank_back[1], bank_back[2], bank_back[0], bank_h1[1], bank_w2[0], bank_w3, bank_h1[0], bank_w2[1]]
        for c in range(QUARTERS):
            project(0, c)
        last_z_rows()
